import numpy as np
import ml_dtypes


def mxq(x, axis, fmt="e4m3"):
    dtype, down = {"e4m3": (ml_dtypes.float8_e4m3fn, 7), "e5m2": (ml_dtypes.float8_e5m2, 14)}[fmt]
    v = np.moveaxis(np.asarray(x, np.float32).astype(ml_dtypes.bfloat16).astype(np.float64), axis, -1)
    blocks = v.reshape(v.shape[:-1] + (-1, 32))
    amax = np.abs(blocks).max(-1, keepdims=True)
    byte = np.maximum(np.where(amax > 0, np.frexp(amax)[1] - 1 + 127, 0) - down, 1)
    scale = np.exp2(byte - 127.0)
    codes = (blocks / scale).astype(np.float32).astype(dtype).astype(np.float64)
    return np.moveaxis((codes * scale).reshape(v.shape), -1, axis)


WIDE = False


def mx_kscale(k):
    if not WIDE:
        return np.ones(k)
    levels = np.array([10, -10, 5, -5, 0])
    if k % 512:
        return np.exp2(np.random.permutation(np.resize(levels, k // 32))).repeat(32)
    a = np.empty((k // 512, 16))
    for p in range(k // 512):
        a[p, :8] = np.random.permutation(np.resize(levels, 8))
        for g in range(8):
            far = levels[np.abs(levels - a[p, g]) >= 10]
            a[p, g + 8] = far[np.random.randint(len(far))]
    return np.exp2(a.ravel()).repeat(32)


def f64(x):
    return np.asarray(x).astype(np.float64)


def striped(idx):
    return np.tile(idx.reshape(-1, 16).T, (8, 1)).astype(np.uint16)


def unstriped(offs):
    return offs[:16].T.reshape(-1).astype(np.int64)


E2M1 = np.array([0.0, 0.5, 1.0, 1.5, 2.0, 3.0, 4.0, 6.0, -0.0, -0.5, -1.0, -1.5, -2.0, -3.0, -4.0, -6.0])


def pack_weight(w, fmt):
    k, n = w.shape
    w = f64(np.asarray(w, np.float32).astype(ml_dtypes.bfloat16)).reshape(k // 32, 32, n)
    amax = np.abs(w).max(1)
    if fmt == "e4m3":
        byte = np.frexp(amax)[1] - 1 + 127 - 7
    else:
        mant, ex = np.frexp(amax / 6.0)
        byte = np.where(mant > 0.5, ex, ex - 1) + 127
    byte = np.clip(np.where(amax > 0, byte, 1), 1, 254)
    scaled = (w * np.exp2(127.0 - byte)[:, None, :]).reshape(k, n).astype(np.float32)
    by_word = np.ascontiguousarray(scaled.reshape(k // 512, 128, 4, n).transpose(0, 1, 3, 2))
    if fmt == "e4m3":
        words = by_word.astype(ml_dtypes.float8_e4m3fn).view(np.uint8)
    else:
        c = by_word.astype(ml_dtypes.float4_e2m1fn).view(np.uint8) & 0xF
        words = (c[..., 0::2] | (c[..., 1::2] << 4)).reshape(k // 512, 128, 2 * n)
    return np.ascontiguousarray(words), np.ascontiguousarray(byte.astype(np.uint8).reshape(k // 512, 16, n))


def unpack_weight(words, scales, fmt):
    g, _, n = scales.shape
    words = np.ascontiguousarray(words).reshape(g, 128, n, -1)
    if fmt == "e4m3":
        vals = words.view(ml_dtypes.float8_e4m3fn).astype(np.float64)
    else:
        nib = np.empty((g, 128, n, 4), np.uint8)
        nib[..., 0::2] = words & 0xF
        nib[..., 1::2] = words >> 4
        vals = E2M1[nib]
    vals = vals * np.repeat(np.exp2(scales.astype(np.float64) - 127.0), 8, axis=1)[..., None]
    return vals.transpose(0, 1, 3, 2).reshape(g * 512, n)


def gelu(v):
    return 0.5 * v * (1.0 + np.tanh(np.sqrt(2.0 / np.pi) * (v + 0.044715 * v**3)))


def striped8(idx):
    return np.concatenate([v.reshape(-1, 16).T for v in idx]).astype(np.uint16)


def unstriped8(offs):
    return np.stack([offs[16 * g:16 * g + 16].T.reshape(-1) for g in range(8)]).astype(np.int64)


def runs(v, idx8):
    k = np.arange(v.shape[0])
    return v[k[:, None], idx8[k % 512 // 64]]


K, T, S, H, N = 512, 2048, 1024, 1024, 256

def setup_inputs():
    n = np.random.standard_normal
    s = mx_kscale(K)[:, None]
    u = mx_kscale(H)[:, None]
    tab_words, tab_scales = pack_weight(n((K, T)) * s, "e4m3")
    offs = striped8(np.stack([np.random.permutation(T)[:S] for _ in range(8)]))
    w1 = (1.5 * n((K, H)) / np.sqrt(K) / s).astype(np.float32)
    w2_words, w2_scales = pack_weight(n((K, H)) / np.sqrt(K) / s, "e2m1")
    w3_words, w3_scales = pack_weight(n((H, N)) / np.sqrt(H) / u, "e4m3")
    gain = (np.exp(0.3 * n(H)) * u[:, 0]).astype(np.float32)
    return {"tab_words": tab_words, "tab_scales": tab_scales, "offs": offs,
            "w1": w1, "w2_words": w2_words, "w2_scales": w2_scales,
            "w3_words": w3_words, "w3_scales": w3_scales, "gain": gain}

def reference(tab_words, tab_scales, offs, w1, w2_words, w2_scales, w3_words, w3_scales, gain):
    v = runs(unpack_weight(tab_words, tab_scales, "e4m3"), unstriped8(offs))
    w2 = unpack_weight(w2_words, w2_scales, "e2m1")
    w3 = unpack_weight(w3_words, w3_scales, "e4m3")
    a = mxq(w1, 0, "e4m3").T @ v
    b = w2.T @ v
    h = f64(gain)[:, None] * (np.log1p(a * a) - np.abs(b))
    y = w3.T @ mxq(h, 0, "e4m3")
    return y * y

@@ -1,0 +1,262 @@
+from contextlib import ExitStack
+
+import concourse.mybir as mybir
+
+K, T, S, H, N = 512, 2048, 1024, 1024, 256
+FLOPS = 2 * K * H * S * 2 + 2 * H * N * S
+
+F32 = mybir.dt.float32
+BF16 = mybir.dt.bfloat16
+I32 = mybir.dt.int32
+U32 = mybir.dt.uint32
+U16 = mybir.dt.uint16
+U8 = mybir.dt.uint8
+FP8X4 = mybir.dt.float8_e4m3fn_x4
+FP4X4 = mybir.dt.float4_e2m1fn_x4
+ACT = mybir.ActivationFunctionType
+ALU = mybir.AluOpType
+
+P = 128
+PACK = 4
+JB = 128
+PAIR = 256
+HALF = 512
+UNITS = [(0, 0), (0, 1), (1, 0), (1, 1), (0, 2), (1, 2), (0, 3), (1, 3)]
+VECTOR_ABS = (2, 3, 4, 5)
+
+
+def tile_list_lightning_flash_layers_kernel(
+    tc, tab_words, tab_scales, offs, w1, w2_words, w2_scales, w3_words, w3_scales, gain, out
+):
+    nc = tc.nc
+    with ExitStack() as ctx:
+        keep = ctx.enter_context(tc.tile_pool(name="keep", bufs=1))
+        work = ctx.enter_context(tc.tile_pool(name="work", bufs=3))
+        psum_a = ctx.enter_context(tc.psum_pool(name="psum_a", bufs=3))
+        psum_b = ctx.enter_context(tc.psum_pool(name="psum_b", bufs=3))
+        psum_y = ctx.enter_context(tc.psum_pool(name="psum_y", bufs=2))
+
+        offsets = keep.tile([P, S // 16], U16, name="offsets")
+        nc.sync.dma_start(offsets[:], offs)
+
+        tab_s = keep.tile([P, T], U8, name="tab_s", tag="tab_s", align_bytes=64)
+        nc.gpsimd.memset(tab_s[:].bitcast(I32), 0)
+        for e in range(2):
+            nc.sync.dma_start(tab_s[e:P:16, :].bitcast(I32), tab_scales[0, e:16:2, :].bitcast(I32))
+
+        warm = keep.tile([P, 2], F32, name="warm")
+        nc.vector.memset(warm[:, 0:1], 1.0)
+        nc.scalar.activation(warm[:, 1:2], warm[:, 0:1], ACT.Ln)
+
+        w1_rows = w1.rearrange("(p i) c -> p i c", i=PACK)
+        w1_raw = []
+
+        def load_w1(c):
+            raw = keep.tile([P, PACK, 256], F32, name="w1_raw", bufs=2)
+            nc.sync.dma_start(raw[:], w1_rows[:, :, 256 * c : 256 * (c + 1)])
+            w1_raw.append(raw)
+
+        load_w1(0)
+        load_w1(1)
+        tab_w = keep.tile([P, T], U32, name="tab_w", align_bytes=64)
+        nc.sync.dma_start(tab_w[:].bitcast(I32), tab_words[0].rearrange("p t i -> p (t i)").bitcast(I32))
+        w2_raw = keep.tile([P, 2 * H], U8, name="w2_raw", align_bytes=64)
+        nc.sync.dma_start(w2_raw[:].bitcast(I32), w2_words[0].bitcast(I32))
+
+        w2_raw_s = keep.tile([P, H], U8, name="w2_raw_s", align_bytes=64)
+        nc.gpsimd.memset(w2_raw_s[:].bitcast(I32), 0)
+        for r in range(4):
+            nc.gpsimd.dma_start(w2_raw_s[r:P:32, :].bitcast(I32), w2_scales[0, r:16:4, :].bitcast(I32))
+        gains = keep.tile([P, 2, PACK], F32, name="gains")
+        nc.gpsimd.dma_start(gains[:], gain.rearrange("(a p t) -> p a t", a=2, t=PACK))
+        w3_s = keep.tile([P, 2, N], U8, name="w3_s", align_bytes=64)
+        nc.gpsimd.memset(w3_s[:].rearrange("p a c -> p (a c)").bitcast(I32), 0)
+        for r in range(4):
+            nc.gpsimd.dma_start(
+                w3_s[r:P:32, :, :].bitcast(I32),
+                w3_scales[:, r:16:4, :].rearrange("a q c -> q a c").bitcast(I32),
+            )
+
+        v_s = []
+
+        def gather_scales(half, queue):
+            picked = keep.tile([P, HALF], U8, name="picked_s%d" % half, align_bytes=64)
+            nc.vector.tensor_copy(picked[:], tab_s[:].indirect(offsets[:, 32 * half : 32 * (half + 1)]))
+            plane = keep.tile([P, HALF], U8, name="v_s%d" % half, align_bytes=64)
+            nc.vector.tensor_copy(plane[:].bitcast(I32), picked[:].bitcast(I32))
+            for e in range(2):
+                queue.dma_start(plane[2 + e : P : 32, :].bitcast(I32), picked[16 + e : P : 32, :].bitcast(I32))
+            v_s.append(plane)
+
+        v_w = []
+
+        def gather_words(pair):
+            picked = keep.tile([P, PAIR], U32, name="v_w%d" % pair, align_bytes=64)
+            nc.vector.tensor_copy(picked[:], tab_w[:].indirect(offsets[:, 16 * pair : 16 * (pair + 1)]))
+            v_w.append(picked)
+
+        w1_bf = [keep.tile([P, PACK, P, PACK], BF16, name="w1_bf%d" % a, align_bytes=64) for a in range(2)]
+        w1_q = [keep.tile([P, 512], U32, name="w1_q%d" % a, align_bytes=64) for a in range(2)]
+        w1_s = [keep.tile([P, 512], U8, name="w1_s%d" % a, align_bytes=64) for a in range(2)]
+
+        def quantize_w1(a):
+            nc.vector.quantize_mx(
+                out=w1_q[a][:].bitcast(FP8X4),
+                scales=w1_s[a][:],
+                in_=w1_bf[a][:].rearrange("p t m i -> p (t m i)"),
+            )
+
+        def cast_w1(c, copy):
+            a, m0 = c // 2, 64 * (c % 2)
+            copy(
+                w1_bf[a][:, :, m0 : m0 + 64, :].rearrange("p t m i -> p m i t"),
+                w1_raw[c][:].rearrange("p i (m t) -> p m i t", t=PACK),
+            )
+
+        gather_scales(0, nc.scalar)
+        for c in range(2):
+            cast_w1(c, nc.scalar.copy)
+            load_w1(c + 2)
+        gather_scales(1, nc.sync)
+        w3_w = keep.tile([P, 2, N], U32, name="w3_w", tag="tab_s", align_bytes=64)
+        nc.sync.dma_start(w3_w[:].bitcast(I32), w3_words.rearrange("a p c i -> p a (c i)").bitcast(I32))
+
+        w2_s = keep.tile([P, H], U8, name="w2_s", align_bytes=64)
+        nc.vector.tensor_copy(
+            w2_s[:].rearrange("p (a t m) -> p a t m", a=2, t=PACK),
+            w2_raw_s[:].rearrange("p (a m t) -> p a t m", a=2, t=PACK),
+        )
+        quantize_w1(0)
+        gather_words(0)
+        w2_w = keep.tile([P, 2 * H], U8, name="w2_w", align_bytes=64)
+        nc.vector.tensor_copy(
+            w2_w[:].bitcast(U16).rearrange("p (a t m) -> p a t m", a=2, t=PACK),
+            w2_raw[:].bitcast(U16).rearrange("p (a m t) -> p a t m", a=2, t=PACK),
+        )
+        gather_words(1)
+
+        h_q = {}
+        h_s = {}
+
+        def products(a, pair, jb):
+            rhs = v_w[pair][:, JB * jb : JB * (jb + 1)].bitcast(FP8X4)
+            j0 = (PAIR * pair + JB * jb) % HALF
+            rhs_scale = v_s[pair // 2][:, j0 : j0 + JB]
+            bank_a = psum_a.tile([P, PACK, JB], F32, name="bank_a")
+            bank_b = psum_b.tile([P, PACK, JB], F32, name="bank_b")
+            for t in range(PACK):
+                nc.tensor.matmul_mx(
+                    out=bank_a[:, t, :],
+                    lhsT=w1_q[a][:, P * t : P * (t + 1)].bitcast(FP8X4),
+                    lhsT_scale=w1_s[a][:, P * t : P * (t + 1)],
+                    rhs=rhs,
+                    rhs_scale=rhs_scale,
+                    start=True,
+                    stop=True,
+                )
+            for t in range(PACK):
+                c0 = 512 * a + P * t
+                nc.tensor.matmul_mx(
+                    out=bank_b[:, t, :],
+                    lhsT=w2_w[:, 2 * c0 : 2 * (c0 + P)].bitcast(FP4X4),
+                    lhsT_scale=w2_s[:, c0 : c0 + P],
+                    rhs=rhs,
+                    rhs_scale=rhs_scale,
+                    start=True,
+                    stop=True,
+                )
+            return bank_a[:].rearrange("p t j -> p j t"), bank_b[:].rearrange("p t j -> p j t")
+
+        def quantize_h(a, pair, h_bf, blocks):
+            if (a, pair) not in h_q:
+                h_q[(a, pair)] = work.tile([P, PAIR], U32, name="h_q", align_bytes=64, bufs=4)
+                h_s[(a, pair)] = work.tile([P, PAIR], U8, name="h_s", align_bytes=64, bufs=4)
+            cols = slice(JB * blocks.start, JB * blocks.stop)
+            nc.vector.quantize_mx(
+                out=h_q[(a, pair)][:, cols].bitcast(FP8X4),
+                scales=h_s[(a, pair)][:, cols],
+                in_=h_bf[:, blocks, :, :].rearrange("p b j t -> p (b j t)"),
+            )
+
+        out_rows = out.rearrange("(b p) j -> p b j", p=P)
+
+        def flash(pair, blocks):
+            cols = slice(JB * blocks.start, JB * blocks.stop)
+            width = cols.stop - cols.start
+            bank_y = psum_y.tile([P, 2, width], F32, name="bank_y")
+            for b in range(2):
+                for a in range(2):
+                    nc.tensor.matmul_mx(
+                        out=bank_y[:, b, :],
+                        lhsT=w3_w[:, a, P * b : P * (b + 1)].bitcast(FP8X4),
+                        lhsT_scale=w3_s[:, a, P * b : P * (b + 1)],
+                        rhs=h_q[(a, pair)][:, cols].bitcast(FP8X4),
+                        rhs_scale=h_s[(a, pair)][:, cols],
+                        start=(a == 0),
+                        stop=(a == 1),
+                    )
+            y2 = work.tile([P, 2, width], F32, name="y2")
+            nc.scalar.activation(y2[:], bank_y[:], ACT.Square)
+            j0 = PAIR * pair + cols.start
+            nc.sync.dma_start(out_rows[:, :, j0 : j0 + width], y2[:])
+
+        both = slice(0, 2)
+        single = [slice(0, 1), slice(1, 2)]
+        pending = None
+        for u, (a, pair) in enumerate(UNITS):
+            banks = [products(a, pair, jb) for jb in range(2)]
+            vector_abs = u in VECTOR_ABS
+            narrow = u in (0, len(UNITS) - 1)
+            sq = work.tile([P, 2, JB, PACK], F32, name="sq")
+            lg = work.tile([P, 2, JB, PACK], F32, name="lg")
+            part = work.tile([P, 2, JB, PACK], F32, name="part")
+            diff = work.tile([P, 2, JB, PACK], F32, name="diff")
+            h_bf = work.tile([P, 2, JB, PACK], BF16, name="h_bf", align_bytes=64)
+            if narrow:
+                for jb in range(2):
+                    nc.scalar.activation(sq[:, jb], banks[jb][0], ACT.Square)
+                    nc.scalar.activation(part[:, jb], banks[jb][1], ACT.Abs)
+                    nc.scalar.activation(lg[:, jb], sq[:, jb], ACT.Ln, bias=1.0)
+            else:
+                for jb in range(2):
+                    nc.scalar.activation(sq[:, jb], banks[jb][0], ACT.Square)
+                nc.scalar.activation(part[:, 1], banks[1][1], ACT.Abs)
+                nc.scalar.activation(lg[:], sq[:], ACT.Ln, bias=1.0)
+                if not vector_abs:
+                    nc.scalar.activation(part[:, 0], banks[0][1], ACT.Abs)
+            g1 = gains[:, a : a + 1, :].broadcast_to([P, JB, PACK])
+            g2 = gains[:, a : a + 1, :].broadcast_to([P, PAIR, PACK])
+            if narrow:
+                nc.vector.tensor_tensor(diff[:, 0], lg[:, 0], part[:, 0], ALU.subtract)
+                if pending is not None:
+                    quantize_h(*pending, both)
+                nc.vector.tensor_tensor(h_bf[:, 0], diff[:, 0], g1, ALU.mult)
+                nc.vector.tensor_tensor(diff[:, 1], lg[:, 1], part[:, 1], ALU.subtract)
+                if u > 0:
+                    quantize_h(a, pair, h_bf, single[0])
+                nc.vector.tensor_tensor(h_bf[:, 1], diff[:, 1], g1, ALU.mult)
+            else:
+                if vector_abs:
+                    nc.vector.scalar_tensor_tensor(part[:, 0], banks[0][1], 0.0, lg[:, 0], ALU.max, ALU.subtract)
+                    nc.vector.tensor_tensor(diff[:, 1], lg[:, 1], part[:, 1], ALU.subtract)
+                    nc.vector.scalar_tensor_tensor(diff[:, 0], banks[0][1], 0.0, part[:, 0], ALU.min, ALU.subtract)
+                else:
+                    nc.vector.tensor_tensor(diff[:], lg[:], part[:], ALU.subtract)
+                quantize_h(*pending, both)
+                nc.vector.tensor_tensor(
+                    h_bf[:].rearrange("p b j t -> p (b j) t"), diff[:].rearrange("p b j t -> p (b j) t"), g2, ALU.mult
+                )
+            if pending is not None and pending[0] == 1:
+                flash(pending[1], both)
+            pending = (a, pair, h_bf)
+            if u == 0:
+                cast_w1(2, nc.vector.tensor_copy)
+                gather_words(2)
+                cast_w1(3, nc.vector.tensor_copy)
+            if u == 1:
+                quantize_w1(1)
+            if u == 2:
+                gather_words(3)
+        flash(pending[1], single[0])
+        quantize_h(*pending, single[1])
+        flash(pending[1], single[1])

@@ -31,44 +31,39 @@ def tile_list_lightning_flash_layers_kernel(
     nc = tc.nc
     with ExitStack() as ctx:
         keep = ctx.enter_context(tc.tile_pool(name="keep", bufs=1))
-        work = ctx.enter_context(tc.tile_pool(name="work", bufs=3))
-        psum_a = ctx.enter_context(tc.psum_pool(name="psum_a", bufs=3))
-        psum_b = ctx.enter_context(tc.psum_pool(name="psum_b", bufs=3))
+        work = ctx.enter_context(tc.tile_pool(name="work", bufs=4))
+        psum_a = ctx.enter_context(tc.psum_pool(name="psum_a", bufs=2))
+        psum_b = ctx.enter_context(tc.psum_pool(name="psum_b", bufs=4))
         psum_y = ctx.enter_context(tc.psum_pool(name="psum_y", bufs=2))
 
         offsets = keep.tile([P, S // 16], U16, name="offsets")
         nc.sync.dma_start(offsets[:], offs)
 
-        tab_s = keep.tile([P, T], U8, name="tab_s", tag="tab_s", align_bytes=64)
+        warm_in = keep.tile([P, 1], F32, name="warm_in", tag="tab_w", align_bytes=64)
+        warm_out = keep.tile([P, 1], F32, name="warm_out", tag="w2_raw_s", align_bytes=64)
+        nc.gpsimd.memset(warm_in[:], 1.0)
+        nc.scalar.activation(warm_out[:], warm_in[:], ACT.Ln)
+
+        tab_s = keep.tile([P, T], U8, name="tab_s", align_bytes=64)
         nc.gpsimd.memset(tab_s[:].bitcast(I32), 0)
         for e in range(2):
             nc.sync.dma_start(tab_s[e:P:16, :].bitcast(I32), tab_scales[0, e:16:2, :].bitcast(I32))
 
-        warm = keep.tile([P, 2], F32, name="warm")
-        nc.vector.memset(warm[:, 0:1], 1.0)
-        nc.scalar.activation(warm[:, 1:2], warm[:, 0:1], ACT.Ln)
-
         w1_rows = w1.rearrange("(p i) c -> p i c", i=PACK)
         w1_raw = []
-
-        def load_w1(c):
-            raw = keep.tile([P, PACK, 256], F32, name="w1_raw", bufs=2)
+        for c in range(2):
+            raw = keep.tile([P, PACK, 256], F32, name="w1_raw%d" % c, tag="w1_raw%d" % c, align_bytes=64)
             nc.sync.dma_start(raw[:], w1_rows[:, :, 256 * c : 256 * (c + 1)])
             w1_raw.append(raw)
-
-        load_w1(0)
-        load_w1(1)
-        tab_w = keep.tile([P, T], U32, name="tab_w", align_bytes=64)
+        tab_w = keep.tile([P, T], U32, name="tab_w", tag="tab_w", align_bytes=64)
         nc.sync.dma_start(tab_w[:].bitcast(I32), tab_words[0].rearrange("p t i -> p (t i)").bitcast(I32))
-        w2_raw = keep.tile([P, 2 * H], U8, name="w2_raw", align_bytes=64)
-        nc.sync.dma_start(w2_raw[:].bitcast(I32), w2_words[0].bitcast(I32))
-
-        w2_raw_s = keep.tile([P, H], U8, name="w2_raw_s", align_bytes=64)
-        nc.gpsimd.memset(w2_raw_s[:].bitcast(I32), 0)
+        w2_raw_s = keep.tile([P, H], U8, name="w2_raw_s", tag="w2_raw_s", align_bytes=64)
+        nc.vector.memset(w2_raw_s[:].bitcast(I32), 0)
         for r in range(4):
-            nc.gpsimd.dma_start(w2_raw_s[r:P:32, :].bitcast(I32), w2_scales[0, r:16:4, :].bitcast(I32))
+            nc.sync.dma_start(w2_raw_s[r:P:32, :].bitcast(I32), w2_scales[0, r:16:4, :].bitcast(I32))
         gains = keep.tile([P, 2, PACK], F32, name="gains")
         nc.gpsimd.dma_start(gains[:], gain.rearrange("(a p t) -> p a t", a=2, t=PACK))
+
         w3_s = keep.tile([P, 2, N], U8, name="w3_s", align_bytes=64)
         nc.gpsimd.memset(w3_s[:].rearrange("p a c -> p (a c)").bitcast(I32), 0)
         for r in range(4):
@@ -77,25 +72,28 @@ def tile_list_lightning_flash_layers_kernel(
                 w3_scales[:, r:16:4, :].rearrange("a q c -> q a c").bitcast(I32),
             )
 
-        v_s = []
+        v_s = {}
 
-        def gather_scales(half, queue):
-            picked = keep.tile([P, HALF], U8, name="picked_s%d" % half, align_bytes=64)
-            nc.vector.tensor_copy(picked[:], tab_s[:].indirect(offsets[:, 32 * half : 32 * (half + 1)]))
-            plane = keep.tile([P, HALF], U8, name="v_s%d" % half, align_bytes=64)
+        def gather_scales(j0, j1, tag):
+            picked = keep.tile([P, j1 - j0], U8, name="picked_s%d" % j0, tag=tag, align_bytes=64)
+            nc.vector.tensor_copy(picked[:], tab_s[:].indirect(offsets[:, j0 // 16 : j1 // 16]))
+            plane = keep.tile([P, j1 - j0], U8, name="v_s%d" % j0, align_bytes=64)
             nc.vector.tensor_copy(plane[:].bitcast(I32), picked[:].bitcast(I32))
             for e in range(2):
-                queue.dma_start(plane[2 + e : P : 32, :].bitcast(I32), picked[16 + e : P : 32, :].bitcast(I32))
-            v_s.append(plane)
+                nc.sync.dma_start(plane[2 + e : P : 32, :].bitcast(I32), picked[16 + e : P : 32, :].bitcast(I32))
+            for j in range(j0, j1, JB):
+                v_s[j] = plane[:, j - j0 : j - j0 + JB]
 
         v_w = []
 
-        def gather_words(pair):
-            picked = keep.tile([P, PAIR], U32, name="v_w%d" % pair, align_bytes=64)
+        def gather_words(pair, tag):
+            picked = keep.tile([P, PAIR], U32, name="v_w%d" % pair, tag=tag, align_bytes=64)
             nc.vector.tensor_copy(picked[:], tab_w[:].indirect(offsets[:, 16 * pair : 16 * (pair + 1)]))
             v_w.append(picked)
 
-        w1_bf = [keep.tile([P, PACK, P, PACK], BF16, name="w1_bf%d" % a, align_bytes=64) for a in range(2)]
+        w1_bf = [
+            keep.tile([P, PACK, P, PACK], BF16, name="w1_bf%d" % a, tag="w1_bf%d" % a, align_bytes=64) for a in range(2)
+        ]
         w1_q = [keep.tile([P, 512], U32, name="w1_q%d" % a, align_bytes=64) for a in range(2)]
         w1_s = [keep.tile([P, 512], U8, name="w1_s%d" % a, align_bytes=64) for a in range(2)]
 
@@ -106,42 +104,45 @@ def tile_list_lightning_flash_layers_kernel(
                 in_=w1_bf[a][:].rearrange("p t m i -> p (t m i)"),
             )
 
-        def cast_w1(c, copy):
-            a, m0 = c // 2, 64 * (c % 2)
-            copy(
-                w1_bf[a][:, :, m0 : m0 + 64, :].rearrange("p t m i -> p m i t"),
+        gather_scales(0, 512, "picked_s")
+        for c in range(2):
+            nc.scalar.copy(
+                w1_bf[0][:, :, 64 * c : 64 * (c + 1), :].rearrange("p t m i -> p m i t"),
                 w1_raw[c][:].rearrange("p i (m t) -> p m i t", t=PACK),
             )
-
-        gather_scales(0, nc.scalar)
-        for c in range(2):
-            cast_w1(c, nc.scalar.copy)
-            load_w1(c + 2)
-        gather_scales(1, nc.sync)
-        w3_w = keep.tile([P, 2, N], U32, name="w3_w", tag="tab_s", align_bytes=64)
-        nc.sync.dma_start(w3_w[:].bitcast(I32), w3_words.rearrange("a p c i -> p a (c i)").bitcast(I32))
-
-        w2_s = keep.tile([P, H], U8, name="w2_s", align_bytes=64)
-        nc.vector.tensor_copy(
-            w2_s[:].rearrange("p (a t m) -> p a t m", a=2, t=PACK),
-            w2_raw_s[:].rearrange("p (a m t) -> p a t m", a=2, t=PACK),
-        )
+        w2_raw = keep.tile([P, 2 * H], U8, name="w2_raw", tag="w1_raw0", align_bytes=64)
+        nc.sync.dma_start(w2_raw[:].bitcast(I32), w2_words[0].bitcast(I32))
         quantize_w1(0)
-        gather_words(0)
+        gather_words(0, "v_w0")
+        w1_late = keep.tile([P, PACK, 512], F32, name="w1_late", tag="w1_raw1", align_bytes=64)
+        nc.sync.dma_start(w1_late[:], w1_rows[:, :, 512:1024])
+
         w2_w = keep.tile([P, 2 * H], U8, name="w2_w", align_bytes=64)
         nc.vector.tensor_copy(
             w2_w[:].bitcast(U16).rearrange("p (a t m) -> p a t m", a=2, t=PACK),
             w2_raw[:].bitcast(U16).rearrange("p (a m t) -> p a t m", a=2, t=PACK),
         )
-        gather_words(1)
+        w2_s = keep.tile([P, H], U8, name="w2_s", align_bytes=64)
+        nc.vector.tensor_copy(
+            w2_s[:].rearrange("p (a t m) -> p a t m", a=2, t=PACK),
+            w2_raw_s[:].rearrange("p (a m t) -> p a t m", a=2, t=PACK),
+        )
+        w3_w = keep.tile([P, 2, N], U32, name="w3_w", tag="w1_bf0", align_bytes=64)
+        nc.sync.dma_start(w3_w[:].bitcast(I32), w3_words.rearrange("a p c i -> p a (c i)").bitcast(I32))
+        gather_words(1, "w2_raw_s")
+        gather_scales(512, 1024, "picked_s")
+        nc.vector.tensor_copy(
+            w1_bf[1][:].rearrange("p t m i -> p m i t"),
+            w1_late[:].rearrange("p i (m t) -> p m i t", t=PACK),
+        )
+        quantize_w1(1)
 
         h_q = {}
         h_s = {}
 
         def products(a, pair, jb):
             rhs = v_w[pair][:, JB * jb : JB * (jb + 1)].bitcast(FP8X4)
-            j0 = (PAIR * pair + JB * jb) % HALF
-            rhs_scale = v_s[pair // 2][:, j0 : j0 + JB]
+            rhs_scale = v_s[PAIR * pair + JB * jb]
             bank_a = psum_a.tile([P, PACK, JB], F32, name="bank_a")
             bank_b = psum_b.tile([P, PACK, JB], F32, name="bank_b")
             for t in range(PACK):
@@ -206,7 +207,7 @@ def tile_list_lightning_flash_layers_kernel(
         for u, (a, pair) in enumerate(UNITS):
             banks = [products(a, pair, jb) for jb in range(2)]
             vector_abs = u in VECTOR_ABS
-            narrow = u in (0, len(UNITS) - 1)
+            narrow = u in (0, 1, 6, 7)
             sq = work.tile([P, 2, JB, PACK], F32, name="sq")
             lg = work.tile([P, 2, JB, PACK], F32, name="lg")
             part = work.tile([P, 2, JB, PACK], F32, name="part")
@@ -215,8 +216,8 @@ def tile_list_lightning_flash_layers_kernel(
             if narrow:
                 for jb in range(2):
                     nc.scalar.activation(sq[:, jb], banks[jb][0], ACT.Square)
-                    nc.scalar.activation(part[:, jb], banks[jb][1], ACT.Abs)
                     nc.scalar.activation(lg[:, jb], sq[:, jb], ACT.Ln, bias=1.0)
+                    nc.scalar.activation(part[:, jb], banks[jb][1], ACT.Abs)
             else:
                 for jb in range(2):
                     nc.scalar.activation(sq[:, jb], banks[jb][0], ACT.Square)
@@ -232,7 +233,7 @@ def tile_list_lightning_flash_layers_kernel(
                     quantize_h(*pending, both)
                 nc.vector.tensor_tensor(h_bf[:, 0], diff[:, 0], g1, ALU.mult)
                 nc.vector.tensor_tensor(diff[:, 1], lg[:, 1], part[:, 1], ALU.subtract)
-                if u > 0:
+                if u == len(UNITS) - 1:
                     quantize_h(a, pair, h_bf, single[0])
                 nc.vector.tensor_tensor(h_bf[:, 1], diff[:, 1], g1, ALU.mult)
             else:
@@ -250,13 +251,9 @@ def tile_list_lightning_flash_layers_kernel(
                 flash(pending[1], both)
             pending = (a, pair, h_bf)
             if u == 0:
-                cast_w1(2, nc.vector.tensor_copy)
-                gather_words(2)
-                cast_w1(3, nc.vector.tensor_copy)
+                gather_words(2, "w1_raw0")
             if u == 1:
-                quantize_w1(1)
-            if u == 2:
-                gather_words(3)
+                gather_words(3, "w1_raw1")
         flash(pending[1], single[0])
         quantize_h(*pending, single[1])
         flash(pending[1], single[1])

@@ -107,8 +107,8 @@ def tile_list_lightning_flash_layers_kernel(
         gather_scales(0, 512, "picked_s")
         for c in range(2):
             nc.scalar.copy(
-                w1_bf[0][:, :, 64 * c : 64 * (c + 1), :].rearrange("p t m i -> p m i t"),
-                w1_raw[c][:].rearrange("p i (m t) -> p m i t", t=PACK),
+                w1_bf[0][:, :, 64 * c : 64 * (c + 1), :].rearrange("p t m i -> p m t i"),
+                w1_raw[c][:].rearrange("p i (m t) -> p m t i", t=PACK),
             )
         w2_raw = keep.tile([P, 2 * H], U8, name="w2_raw", tag="w1_raw0", align_bytes=64)
         nc.sync.dma_start(w2_raw[:].bitcast(I32), w2_words[0].bitcast(I32))
@@ -132,8 +132,8 @@ def tile_list_lightning_flash_layers_kernel(
         gather_words(1, "w2_raw_s")
         gather_scales(512, 1024, "picked_s")
         nc.vector.tensor_copy(
-            w1_bf[1][:].rearrange("p t m i -> p m i t"),
-            w1_late[:].rearrange("p i (m t) -> p m i t", t=PACK),
+            w1_bf[1][:].rearrange("p t m i -> p m t i"),
+            w1_late[:].rearrange("p i (m t) -> p m t i", t=PACK),
         )
         quantize_w1(1)
 

@@ -23,6 +23,7 @@ PAIR = 256
 HALF = 512
 UNITS = [(0, 0), (0, 1), (1, 0), (1, 1), (0, 2), (1, 2), (0, 3), (1, 3)]
 VECTOR_ABS = (2, 3, 4, 5)
+NARROW = (0, 1, 6, 7)
 
 
 def tile_list_lightning_flash_layers_kernel(
@@ -44,7 +45,7 @@ def tile_list_lightning_flash_layers_kernel(
         nc.gpsimd.memset(warm_in[:], 1.0)
         nc.scalar.activation(warm_out[:], warm_in[:], ACT.Ln)
 
-        tab_s = keep.tile([P, T], U8, name="tab_s", align_bytes=64)
+        tab_s = keep.tile([P, T], U8, name="tab_s", tag="tab_s", align_bytes=64)
         nc.gpsimd.memset(tab_s[:].bitcast(I32), 0)
         for e in range(2):
             nc.sync.dma_start(tab_s[e:P:16, :].bitcast(I32), tab_scales[0, e:16:2, :].bitcast(I32))
@@ -61,16 +62,6 @@ def tile_list_lightning_flash_layers_kernel(
         nc.vector.memset(w2_raw_s[:].bitcast(I32), 0)
         for r in range(4):
             nc.sync.dma_start(w2_raw_s[r:P:32, :].bitcast(I32), w2_scales[0, r:16:4, :].bitcast(I32))
-        gains = keep.tile([P, 2, PACK], F32, name="gains")
-        nc.gpsimd.dma_start(gains[:], gain.rearrange("(a p t) -> p a t", a=2, t=PACK))
-
-        w3_s = keep.tile([P, 2, N], U8, name="w3_s", align_bytes=64)
-        nc.gpsimd.memset(w3_s[:].rearrange("p a c -> p (a c)").bitcast(I32), 0)
-        for r in range(4):
-            nc.gpsimd.dma_start(
-                w3_s[r:P:32, :, :].bitcast(I32),
-                w3_scales[:, r:16:4, :].rearrange("a q c -> q a c").bitcast(I32),
-            )
 
         v_s = {}
 
@@ -127,10 +118,19 @@ def tile_list_lightning_flash_layers_kernel(
             w2_s[:].rearrange("p (a t m) -> p a t m", a=2, t=PACK),
             w2_raw_s[:].rearrange("p (a m t) -> p a t m", a=2, t=PACK),
         )
-        w3_w = keep.tile([P, 2, N], U32, name="w3_w", tag="w1_bf0", align_bytes=64)
-        nc.sync.dma_start(w3_w[:].bitcast(I32), w3_words.rearrange("a p c i -> p a (c i)").bitcast(I32))
+        gains = keep.tile([P, 2, PACK], F32, name="gains", tag="w1_bf0", align_bytes=64)
+        nc.scalar.dma_start(gains[:], gain.rearrange("(a p t) -> p a t", a=2, t=PACK))
         gather_words(1, "w2_raw_s")
         gather_scales(512, 1024, "picked_s")
+        w3_w = keep.tile([P, 2, N], U32, name="w3_w", tag="tab_s", align_bytes=64)
+        nc.sync.dma_start(w3_w[:].bitcast(I32), w3_words.rearrange("a p c i -> p a (c i)").bitcast(I32))
+        w3_s = keep.tile([P, 2, N], U8, name="w3_s", tag="picked_s", align_bytes=64)
+        nc.gpsimd.memset(w3_s[:].rearrange("p a c -> p (a c)").bitcast(I32), 0)
+        for r in range(4):
+            nc.sync.dma_start(
+                w3_s[r:P:32, :, :].bitcast(I32),
+                w3_scales[:, r:16:4, :].rearrange("a q c -> q a c").bitcast(I32),
+            )
         nc.vector.tensor_copy(
             w1_bf[1][:].rearrange("p t m i -> p m t i"),
             w1_late[:].rearrange("p i (m t) -> p m t i", t=PACK),
@@ -140,7 +140,7 @@ def tile_list_lightning_flash_layers_kernel(
         h_q = {}
         h_s = {}
 
-        def products(a, pair, jb):
+        def products(a, pair, jb, order):
             rhs = v_w[pair][:, JB * jb : JB * (jb + 1)].bitcast(FP8X4)
             rhs_scale = v_s[PAIR * pair + JB * jb]
             bank_a = psum_a.tile([P, PACK, JB], F32, name="bank_a")
@@ -166,7 +166,7 @@ def tile_list_lightning_flash_layers_kernel(
                     start=True,
                     stop=True,
                 )
-            return bank_a[:].rearrange("p t j -> p j t"), bank_b[:].rearrange("p t j -> p j t")
+            return bank_a[:].rearrange(order, e=2), bank_b[:].rearrange(order, e=2)
 
         def quantize_h(a, pair, h_bf, blocks):
             if (a, pair) not in h_q:
@@ -181,7 +181,7 @@ def tile_list_lightning_flash_layers_kernel(
 
         out_rows = out.rearrange("(b p) j -> p b j", p=P)
 
-        def flash(pair, blocks):
+        def flash(pair, blocks, queue):
             cols = slice(JB * blocks.start, JB * blocks.stop)
             width = cols.stop - cols.start
             bank_y = psum_y.tile([P, 2, width], F32, name="bank_y")
@@ -199,61 +199,64 @@ def tile_list_lightning_flash_layers_kernel(
             y2 = work.tile([P, 2, width], F32, name="y2")
             nc.scalar.activation(y2[:], bank_y[:], ACT.Square)
             j0 = PAIR * pair + cols.start
-            nc.sync.dma_start(out_rows[:, :, j0 : j0 + width], y2[:])
+            queue.dma_start(out_rows[:, :, j0 : j0 + width], y2[:])
 
         both = slice(0, 2)
         single = [slice(0, 1), slice(1, 2)]
+        last = len(UNITS) - 1
         pending = None
         for u, (a, pair) in enumerate(UNITS):
-            banks = [products(a, pair, jb) for jb in range(2)]
             vector_abs = u in VECTOR_ABS
-            narrow = u in (0, 1, 6, 7)
-            sq = work.tile([P, 2, JB, PACK], F32, name="sq")
-            lg = work.tile([P, 2, JB, PACK], F32, name="lg")
-            part = work.tile([P, 2, JB, PACK], F32, name="part")
-            diff = work.tile([P, 2, JB, PACK], F32, name="diff")
+            narrow = u in NARROW
+            banks = [
+                products(a, pair, 0, "p t (k e) -> p k e t" if vector_abs else "p t (k e) -> p k t e"),
+                products(a, pair, 1, "p t (k e) -> p k t e"),
+            ]
+            sq = work.tile([P, 2, JB // 2, PACK, 2], F32, name="sq")
+            lg = work.tile([P, 2, JB // 2, PACK, 2], F32, name="lg")
+            part = work.tile([P, 2, JB // 2, PACK, 2], F32, name="part")
+            diff = work.tile([P, 2, JB // 2, PACK, 2], F32, name="diff")
             h_bf = work.tile([P, 2, JB, PACK], BF16, name="h_bf", align_bytes=64)
+            gain1 = gains[:, a : a + 1, :].unsqueeze(1).broadcast_to([P, JB // 2, 2, PACK])
+
+            def plain(tile, jb):
+                return tile[:, jb].rearrange("p k t e -> p (k t e)").rearrange("p (k e t) -> p k e t", e=2, t=PACK)
+
+            def scale(jb, woven):
+                source = plain(diff, jb) if woven else diff[:, jb].rearrange("p k t e -> p k e t")
+                nc.vector.tensor_tensor(h_bf[:, jb].rearrange("p (k e) t -> p k e t", e=2), source, gain1, ALU.mult)
+
             if narrow:
                 for jb in range(2):
                     nc.scalar.activation(sq[:, jb], banks[jb][0], ACT.Square)
                     nc.scalar.activation(lg[:, jb], sq[:, jb], ACT.Ln, bias=1.0)
                     nc.scalar.activation(part[:, jb], banks[jb][1], ACT.Abs)
-            else:
-                for jb in range(2):
-                    nc.scalar.activation(sq[:, jb], banks[jb][0], ACT.Square)
-                nc.scalar.activation(part[:, 1], banks[1][1], ACT.Abs)
-                nc.scalar.activation(lg[:], sq[:], ACT.Ln, bias=1.0)
-                if not vector_abs:
-                    nc.scalar.activation(part[:, 0], banks[0][1], ACT.Abs)
-            g1 = gains[:, a : a + 1, :].broadcast_to([P, JB, PACK])
-            g2 = gains[:, a : a + 1, :].broadcast_to([P, PAIR, PACK])
-            if narrow:
                 nc.vector.tensor_tensor(diff[:, 0], lg[:, 0], part[:, 0], ALU.subtract)
                 if pending is not None:
                     quantize_h(*pending, both)
-                nc.vector.tensor_tensor(h_bf[:, 0], diff[:, 0], g1, ALU.mult)
+                scale(0, False)
                 nc.vector.tensor_tensor(diff[:, 1], lg[:, 1], part[:, 1], ALU.subtract)
-                if u == len(UNITS) - 1:
+                if u == last:
                     quantize_h(a, pair, h_bf, single[0])
-                nc.vector.tensor_tensor(h_bf[:, 1], diff[:, 1], g1, ALU.mult)
+                scale(1, False)
             else:
-                if vector_abs:
-                    nc.vector.scalar_tensor_tensor(part[:, 0], banks[0][1], 0.0, lg[:, 0], ALU.max, ALU.subtract)
-                    nc.vector.tensor_tensor(diff[:, 1], lg[:, 1], part[:, 1], ALU.subtract)
-                    nc.vector.scalar_tensor_tensor(diff[:, 0], banks[0][1], 0.0, part[:, 0], ALU.min, ALU.subtract)
-                else:
-                    nc.vector.tensor_tensor(diff[:], lg[:], part[:], ALU.subtract)
+                nc.scalar.activation(plain(sq, 0), banks[0][0], ACT.Square)
+                nc.scalar.activation(sq[:, 1], banks[1][0], ACT.Square)
+                nc.scalar.activation(part[:, 1], banks[1][1], ACT.Abs)
+                nc.scalar.activation(lg[:], sq[:], ACT.Ln, bias=1.0)
+                nc.vector.scalar_tensor_tensor(plain(part, 0), banks[0][1], 0.0, plain(lg, 0), ALU.max, ALU.subtract)
+                nc.vector.tensor_tensor(diff[:, 1], lg[:, 1], part[:, 1], ALU.subtract)
+                nc.vector.scalar_tensor_tensor(plain(diff, 0), banks[0][1], 0.0, plain(part, 0), ALU.min, ALU.subtract)
+                scale(1, False)
                 quantize_h(*pending, both)
-                nc.vector.tensor_tensor(
-                    h_bf[:].rearrange("p b j t -> p (b j) t"), diff[:].rearrange("p b j t -> p (b j) t"), g2, ALU.mult
-                )
+                scale(0, True)
             if pending is not None and pending[0] == 1:
-                flash(pending[1], both)
+                flash(pending[1], both, nc.sync)
             pending = (a, pair, h_bf)
             if u == 0:
                 gather_words(2, "w1_raw0")
             if u == 1:
                 gather_words(3, "w1_raw1")
-        flash(pending[1], single[0])
+        flash(pending[1], single[0], nc.sync)
         quantize_h(*pending, single[1])
-        flash(pending[1], single[1])
+        flash(pending[1], single[1], nc.scalar)

@@ -3,7 +3,7 @@ from contextlib import ExitStack
 import concourse.mybir as mybir
 
 K, T, S, H, N = 512, 2048, 1024, 1024, 256
-FLOPS = 2 * K * H * S * 2 + 2 * H * N * S
+FLOPS = 2 * (2 * K * H * S) + 2 * H * N * S
 
 F32 = mybir.dt.float32
 BF16 = mybir.dt.bfloat16
@@ -18,12 +18,15 @@ ALU = mybir.AluOpType
 
 P = 128
 PACK = 4
-JB = 128
-PAIR = 256
-HALF = 512
-UNITS = [(0, 0), (0, 1), (1, 0), (1, 1), (0, 2), (1, 2), (0, 3), (1, 3)]
-VECTOR_ABS = (2, 3, 4, 5)
-NARROW = (0, 1, 6, 7)
+PASS = P * PACK
+BLOCK = 128
+PAIR = 2 * BLOCK
+HALF = S // 2
+GROUP = 16
+ALIGN = 64
+STEPS = [(0, 0), (0, 1), (1, 0), (1, 1), (0, 2), (1, 2), (0, 3), (1, 3)]
+VECTOR_ABS_STEPS = range(1, 5)
+WORK_BUFS = 4
 
 
 def tile_list_lightning_flash_layers_kernel(
@@ -32,119 +35,112 @@ def tile_list_lightning_flash_layers_kernel(
     nc = tc.nc
     with ExitStack() as ctx:
         keep = ctx.enter_context(tc.tile_pool(name="keep", bufs=1))
-        work = ctx.enter_context(tc.tile_pool(name="work", bufs=4))
+        work = ctx.enter_context(tc.tile_pool(name="work", bufs=WORK_BUFS))
         psum_a = ctx.enter_context(tc.psum_pool(name="psum_a", bufs=2))
         psum_b = ctx.enter_context(tc.psum_pool(name="psum_b", bufs=4))
         psum_y = ctx.enter_context(tc.psum_pool(name="psum_y", bufs=2))
 
-        offsets = keep.tile([P, S // 16], U16, name="offsets")
+        def held(shape, dtype, name, after=None):
+            return keep.tile(shape, dtype, name=name, tag=after or name, align_bytes=ALIGN)
+
+        offsets = keep.tile([P, S // GROUP], U16, name="offsets")
         nc.sync.dma_start(offsets[:], offs)
 
-        warm_in = keep.tile([P, 1], F32, name="warm_in", tag="tab_w", align_bytes=64)
-        warm_out = keep.tile([P, 1], F32, name="warm_out", tag="w2_raw_s", align_bytes=64)
+        warm_in = held([P, 1], F32, "warm_in")
+        warm_out = held([P, 1], F32, "warm_out")
         nc.gpsimd.memset(warm_in[:], 1.0)
         nc.scalar.activation(warm_out[:], warm_in[:], ACT.Ln)
 
-        tab_s = keep.tile([P, T], U8, name="tab_s", tag="tab_s", align_bytes=64)
+        tab_s = held([P, T], U8, "tab_s")
         nc.gpsimd.memset(tab_s[:].bitcast(I32), 0)
         for e in range(2):
-            nc.sync.dma_start(tab_s[e:P:16, :].bitcast(I32), tab_scales[0, e:16:2, :].bitcast(I32))
+            nc.sync.dma_start(tab_s[e:P:GROUP, :].bitcast(I32), tab_scales[0, e:16:2, :].bitcast(I32))
 
         w1_rows = w1.rearrange("(p i) c -> p i c", i=PACK)
-        w1_raw = []
+        w1_piece = [held([P, PACK, PASS // 2], F32, "w1_piece%d" % c) for c in range(2)]
         for c in range(2):
-            raw = keep.tile([P, PACK, 256], F32, name="w1_raw%d" % c, tag="w1_raw%d" % c, align_bytes=64)
-            nc.sync.dma_start(raw[:], w1_rows[:, :, 256 * c : 256 * (c + 1)])
-            w1_raw.append(raw)
-        tab_w = keep.tile([P, T], U32, name="tab_w", tag="tab_w", align_bytes=64)
+            nc.sync.dma_start(w1_piece[c][:], w1_rows[:, :, PASS // 2 * c : PASS // 2 * (c + 1)])
+        tab_w = held([P, T], U32, "tab_w", after="warm_in")
         nc.sync.dma_start(tab_w[:].bitcast(I32), tab_words[0].rearrange("p t i -> p (t i)").bitcast(I32))
-        w2_raw_s = keep.tile([P, H], U8, name="w2_raw_s", tag="w2_raw_s", align_bytes=64)
-        nc.vector.memset(w2_raw_s[:].bitcast(I32), 0)
+
+        w2_in = held([P, 3 * H], U8, "w2_in", after="warm_out")
+        w2_in_w = w2_in[:, : 2 * H]
+        w2_in_s = w2_in[:, 2 * H :]
+        nc.sync.dma_start(w2_in_w.bitcast(I32), w2_words[0].bitcast(I32))
+        nc.gpsimd.memset(w2_in_s.bitcast(I32), 0)
         for r in range(4):
-            nc.sync.dma_start(w2_raw_s[r:P:32, :].bitcast(I32), w2_scales[0, r:16:4, :].bitcast(I32))
+            nc.sync.dma_start(w2_in_s[r:P:32, :].bitcast(I32), w2_scales[0, r:16:4, :].bitcast(I32))
 
-        v_s = {}
-
-        def gather_scales(j0, j1, tag):
-            picked = keep.tile([P, j1 - j0], U8, name="picked_s%d" % j0, tag=tag, align_bytes=64)
-            nc.vector.tensor_copy(picked[:], tab_s[:].indirect(offsets[:, j0 // 16 : j1 // 16]))
-            plane = keep.tile([P, j1 - j0], U8, name="v_s%d" % j0, align_bytes=64)
-            nc.vector.tensor_copy(plane[:].bitcast(I32), picked[:].bitcast(I32))
+        def gather_scales(half, after):
+            picked = held([P, HALF], U8, "picked_s%d" % half, after=after)
+            columns = slice(HALF // GROUP * half, HALF // GROUP * (half + 1))
+            nc.vector.tensor_copy(picked[:], tab_s[:].indirect(offsets[:, columns]))
+            placed = held([P, HALF], U8, "v_s%d" % half)
+            nc.vector.tensor_copy(placed[:].bitcast(I32), picked[:].bitcast(I32))
             for e in range(2):
-                nc.sync.dma_start(plane[2 + e : P : 32, :].bitcast(I32), picked[16 + e : P : 32, :].bitcast(I32))
-            for j in range(j0, j1, JB):
-                v_s[j] = plane[:, j - j0 : j - j0 + JB]
+                nc.sync.dma_start(placed[2 + e : P : 32, :].bitcast(I32), picked[GROUP + e : P : 32, :].bitcast(I32))
+            return placed
 
-        v_w = []
+        def gather_words(pair, after):
+            picked = held([P, PAIR], U32, "v_w%d" % pair, after=after)
+            columns = slice(PAIR // GROUP * pair, PAIR // GROUP * (pair + 1))
+            nc.vector.tensor_copy(picked[:], tab_w[:].indirect(offsets[:, columns]))
+            return picked
 
-        def gather_words(pair, tag):
-            picked = keep.tile([P, PAIR], U32, name="v_w%d" % pair, tag=tag, align_bytes=64)
-            nc.vector.tensor_copy(picked[:], tab_w[:].indirect(offsets[:, 16 * pair : 16 * (pair + 1)]))
-            v_w.append(picked)
+        w1_bf = [held([P, PACK, P, PACK], BF16, "w1_bf%d" % a) for a in range(2)]
+        w1_q = [held([P, PASS], U32, "w1_q%d" % a) for a in range(2)]
+        w1_s = [held([P, PASS], U8, "w1_s%d" % a) for a in range(2)]
 
-        w1_bf = [
-            keep.tile([P, PACK, P, PACK], BF16, name="w1_bf%d" % a, tag="w1_bf%d" % a, align_bytes=64) for a in range(2)
-        ]
-        w1_q = [keep.tile([P, 512], U32, name="w1_q%d" % a, align_bytes=64) for a in range(2)]
-        w1_s = [keep.tile([P, 512], U8, name="w1_s%d" % a, align_bytes=64) for a in range(2)]
+        def cast_w1(copy, target, source):
+            copy(target.rearrange("p t m i -> p m t i"), source.rearrange("p i (m t) -> p m t i", t=PACK))
 
         def quantize_w1(a):
             nc.vector.quantize_mx(
-                out=w1_q[a][:].bitcast(FP8X4),
-                scales=w1_s[a][:],
-                in_=w1_bf[a][:].rearrange("p t m i -> p (t m i)"),
+                out=w1_q[a][:].bitcast(FP8X4), scales=w1_s[a][:], in_=w1_bf[a][:].rearrange("p t m i -> p (t m i)")
             )
 
-        gather_scales(0, 512, "picked_s")
+        v_s = [gather_scales(0, None)]
         for c in range(2):
-            nc.scalar.copy(
-                w1_bf[0][:, :, 64 * c : 64 * (c + 1), :].rearrange("p t m i -> p m t i"),
-                w1_raw[c][:].rearrange("p i (m t) -> p m t i", t=PACK),
-            )
-        w2_raw = keep.tile([P, 2 * H], U8, name="w2_raw", tag="w1_raw0", align_bytes=64)
-        nc.sync.dma_start(w2_raw[:].bitcast(I32), w2_words[0].bitcast(I32))
+            cast_w1(nc.scalar.copy, w1_bf[0][:, :, P // 2 * c : P // 2 * (c + 1), :], w1_piece[c][:])
+        v_s.append(gather_scales(1, "w1_piece0"))
         quantize_w1(0)
-        gather_words(0, "v_w0")
-        w1_late = keep.tile([P, PACK, 512], F32, name="w1_late", tag="w1_raw1", align_bytes=64)
-        nc.sync.dma_start(w1_late[:], w1_rows[:, :, 512:1024])
+        v_w = [gather_words(0, None)]
+        w1_late = held([P, PACK, PASS], F32, "w1_late", after="w1_piece1")
+        nc.sync.dma_start(w1_late[:], w1_rows[:, :, PASS:])
 
-        w2_w = keep.tile([P, 2 * H], U8, name="w2_w", align_bytes=64)
+        w2_w = held([P, 2 * H], U8, "w2_w")
         nc.vector.tensor_copy(
             w2_w[:].bitcast(U16).rearrange("p (a t m) -> p a t m", a=2, t=PACK),
-            w2_raw[:].bitcast(U16).rearrange("p (a m t) -> p a t m", a=2, t=PACK),
+            w2_in_w.bitcast(U16).rearrange("p (a m t) -> p a t m", a=2, t=PACK),
         )
-        w2_s = keep.tile([P, H], U8, name="w2_s", align_bytes=64)
+        w2_s = held([P, H], U8, "w2_s")
         nc.vector.tensor_copy(
             w2_s[:].rearrange("p (a t m) -> p a t m", a=2, t=PACK),
-            w2_raw_s[:].rearrange("p (a m t) -> p a t m", a=2, t=PACK),
+            w2_in_s.rearrange("p (a m t) -> p a t m", a=2, t=PACK),
         )
-        gains = keep.tile([P, 2, PACK], F32, name="gains", tag="w1_bf0", align_bytes=64)
-        nc.scalar.dma_start(gains[:], gain.rearrange("(a p t) -> p a t", a=2, t=PACK))
-        gather_words(1, "w2_raw_s")
-        gather_scales(512, 1024, "picked_s")
-        w3_w = keep.tile([P, 2, N], U32, name="w3_w", tag="tab_s", align_bytes=64)
+        v_w.append(gather_words(1, "warm_out"))
+        v_w.append(gather_words(2, "picked_s0"))
+        v_w.append(gather_words(3, "w1_bf0"))
+
+        gains = held([P, 2, PACK], F32, "gains", after="tab_s")
+        nc.sync.dma_start(gains[:], gain.rearrange("(a p t) -> p a t", a=2, t=PACK))
+        w3_w = held([P, 2, N], U32, "w3_w", after="w1_piece1")
         nc.sync.dma_start(w3_w[:].bitcast(I32), w3_words.rearrange("a p c i -> p a (c i)").bitcast(I32))
-        w3_s = keep.tile([P, 2, N], U8, name="w3_s", tag="picked_s", align_bytes=64)
+        w3_s = held([P, 2, N], U8, "w3_s", after="w1_piece0")
         nc.gpsimd.memset(w3_s[:].rearrange("p a c -> p (a c)").bitcast(I32), 0)
         for r in range(4):
             nc.sync.dma_start(
-                w3_s[r:P:32, :, :].bitcast(I32),
-                w3_scales[:, r:16:4, :].rearrange("a q c -> q a c").bitcast(I32),
+                w3_s[r:P:32, :, :].bitcast(I32), w3_scales[:, r:16:4, :].rearrange("a q c -> q a c").bitcast(I32)
             )
-        nc.vector.tensor_copy(
-            w1_bf[1][:].rearrange("p t m i -> p m t i"),
-            w1_late[:].rearrange("p i (m t) -> p m t i", t=PACK),
-        )
+        cast_w1(nc.vector.tensor_copy, w1_bf[1][:], w1_late[:])
         quantize_w1(1)
 
-        h_q = {}
-        h_s = {}
-
-        def products(a, pair, jb, order):
-            rhs = v_w[pair][:, JB * jb : JB * (jb + 1)].bitcast(FP8X4)
-            rhs_scale = v_s[PAIR * pair + JB * jb]
-            bank_a = psum_a.tile([P, PACK, JB], F32, name="bank_a")
-            bank_b = psum_b.tile([P, PACK, JB], F32, name="bank_b")
+        def products(a, pair, block):
+            rhs = v_w[pair][:, BLOCK * block : BLOCK * (block + 1)].bitcast(FP8X4)
+            half, j0 = divmod(PAIR * pair + BLOCK * block, HALF)
+            rhs_scale = v_s[half][:, j0 : j0 + BLOCK]
+            bank_a = psum_a.tile([P, PACK, BLOCK], F32, name="bank_a")
+            bank_b = psum_b.tile([P, PACK, BLOCK], F32, name="bank_b")
             for t in range(PACK):
                 nc.tensor.matmul_mx(
                     out=bank_a[:, t, :],
@@ -156,7 +152,7 @@ def tile_list_lightning_flash_layers_kernel(
                     stop=True,
                 )
             for t in range(PACK):
-                c0 = 512 * a + P * t
+                c0 = PASS * a + P * t
                 nc.tensor.matmul_mx(
                     out=bank_b[:, t, :],
                     lhsT=w2_w[:, 2 * c0 : 2 * (c0 + P)].bitcast(FP4X4),
@@ -166,97 +162,95 @@ def tile_list_lightning_flash_layers_kernel(
                     start=True,
                     stop=True,
                 )
-            return bank_a[:].rearrange(order, e=2), bank_b[:].rearrange(order, e=2)
+            return bank_a[:].rearrange("p t j -> p j t"), bank_b[:].rearrange("p t j -> p j t")
 
-        def quantize_h(a, pair, h_bf, blocks):
-            if (a, pair) not in h_q:
-                h_q[(a, pair)] = work.tile([P, PAIR], U32, name="h_q", align_bytes=64, bufs=4)
-                h_s[(a, pair)] = work.tile([P, PAIR], U8, name="h_s", align_bytes=64, bufs=4)
-            cols = slice(JB * blocks.start, JB * blocks.stop)
+        h_bf = {}
+        h_q = {}
+        h_s = {}
+
+        def quantize_h(step, entries):
             nc.vector.quantize_mx(
-                out=h_q[(a, pair)][:, cols].bitcast(FP8X4),
-                scales=h_s[(a, pair)][:, cols],
-                in_=h_bf[:, blocks, :, :].rearrange("p b j t -> p (b j t)"),
+                out=h_q[step][:, entries].bitcast(FP8X4),
+                scales=h_s[step][:, entries],
+                in_=h_bf[step][:, entries, :].rearrange("p j t -> p (j t)"),
             )
 
-        out_rows = out.rearrange("(b p) j -> p b j", p=P)
+        out_rows = out.rearrange("(c p) j -> p c j", p=P)
 
-        def flash(pair, blocks, queue):
-            cols = slice(JB * blocks.start, JB * blocks.stop)
-            width = cols.stop - cols.start
+        def flash(pair, entries, queue):
+            width = entries.stop - entries.start
             bank_y = psum_y.tile([P, 2, width], F32, name="bank_y")
-            for b in range(2):
+            for c in range(2):
                 for a in range(2):
                     nc.tensor.matmul_mx(
-                        out=bank_y[:, b, :],
-                        lhsT=w3_w[:, a, P * b : P * (b + 1)].bitcast(FP8X4),
-                        lhsT_scale=w3_s[:, a, P * b : P * (b + 1)],
-                        rhs=h_q[(a, pair)][:, cols].bitcast(FP8X4),
-                        rhs_scale=h_s[(a, pair)][:, cols],
+                        out=bank_y[:, c, :],
+                        lhsT=w3_w[:, a, P * c : P * (c + 1)].bitcast(FP8X4),
+                        lhsT_scale=w3_s[:, a, P * c : P * (c + 1)],
+                        rhs=h_q[(a, pair)][:, entries].bitcast(FP8X4),
+                        rhs_scale=h_s[(a, pair)][:, entries],
                         start=(a == 0),
                         stop=(a == 1),
                     )
-            y2 = work.tile([P, 2, width], F32, name="y2")
-            nc.scalar.activation(y2[:], bank_y[:], ACT.Square)
-            j0 = PAIR * pair + cols.start
-            queue.dma_start(out_rows[:, :, j0 : j0 + width], y2[:])
+            squared = work.tile([P, 2, width], F32, name="squared")
+            nc.scalar.activation(squared[:], bank_y[:], ACT.Square)
+            j0 = PAIR * pair + entries.start
+            queue.dma_start(out_rows[:, :, j0 : j0 + width], squared[:])
 
-        both = slice(0, 2)
-        single = [slice(0, 1), slice(1, 2)]
-        last = len(UNITS) - 1
-        pending = None
-        for u, (a, pair) in enumerate(UNITS):
-            vector_abs = u in VECTOR_ABS
-            narrow = u in NARROW
-            banks = [
-                products(a, pair, 0, "p t (k e) -> p k e t" if vector_abs else "p t (k e) -> p k t e"),
-                products(a, pair, 1, "p t (k e) -> p k t e"),
-            ]
-            sq = work.tile([P, 2, JB // 2, PACK, 2], F32, name="sq")
-            lg = work.tile([P, 2, JB // 2, PACK, 2], F32, name="lg")
-            part = work.tile([P, 2, JB // 2, PACK, 2], F32, name="part")
-            diff = work.tile([P, 2, JB // 2, PACK, 2], F32, name="diff")
-            h_bf = work.tile([P, 2, JB, PACK], BF16, name="h_bf", align_bytes=64)
-            gain1 = gains[:, a : a + 1, :].unsqueeze(1).broadcast_to([P, JB // 2, 2, PACK])
+        whole = slice(0, PAIR)
+        blocks = [slice(0, BLOCK), slice(BLOCK, PAIR)]
+        last_halves = [slice(BLOCK, BLOCK + BLOCK // 2), slice(BLOCK + BLOCK // 2, PAIR)]
+        previous = None
+        for u, step in enumerate(STEPS):
+            a, pair = step
+            (a0, b0), (a1, b1) = [products(a, pair, block) for block in range(2)]
+            square = work.tile([P, PAIR, PACK], F32, name="square")
+            logarithm = work.tile([P, PAIR, PACK], F32, name="logarithm")
+            loss = work.tile([P, PAIR, PACK], F32, name="loss")
+            difference = work.tile([P, PAIR, PACK], F32, name="difference")
+            h_bf[step] = work.tile([P, PAIR, PACK], BF16, name="h_bf", align_bytes=ALIGN)
+            h_q[step] = work.tile([P, PAIR], U32, name="h_q", align_bytes=ALIGN)
+            h_s[step] = work.tile([P, PAIR], U8, name="h_s", align_bytes=ALIGN)
 
-            def plain(tile, jb):
-                return tile[:, jb].rearrange("p k t e -> p (k t e)").rearrange("p (k e t) -> p k e t", e=2, t=PACK)
+            def log(entries):
+                nc.scalar.activation(logarithm[:, entries], square[:, entries], ACT.Ln, bias=1.0)
 
-            def scale(jb, woven):
-                source = plain(diff, jb) if woven else diff[:, jb].rearrange("p k t e -> p k e t")
-                nc.vector.tensor_tensor(h_bf[:, jb].rearrange("p (k e) t -> p k e t", e=2), source, gain1, ALU.mult)
+            def subtract(entries):
+                nc.vector.tensor_tensor(difference[:, entries], logarithm[:, entries], loss[:, entries], ALU.subtract)
 
-            if narrow:
-                for jb in range(2):
-                    nc.scalar.activation(sq[:, jb], banks[jb][0], ACT.Square)
-                    nc.scalar.activation(lg[:, jb], sq[:, jb], ACT.Ln, bias=1.0)
-                    nc.scalar.activation(part[:, jb], banks[jb][1], ACT.Abs)
-                nc.vector.tensor_tensor(diff[:, 0], lg[:, 0], part[:, 0], ALU.subtract)
-                if pending is not None:
-                    quantize_h(*pending, both)
-                scale(0, False)
-                nc.vector.tensor_tensor(diff[:, 1], lg[:, 1], part[:, 1], ALU.subtract)
-                if u == last:
-                    quantize_h(a, pair, h_bf, single[0])
-                scale(1, False)
+            def scale(entries):
+                by_slot = gains[:, a : a + 1, :].broadcast_to([P, entries.stop - entries.start, PACK])
+                nc.vector.tensor_tensor(h_bf[step][:, entries], difference[:, entries], by_slot, ALU.mult)
+
+            first, second = blocks
+            nc.scalar.activation(square[:, first], a0, ACT.Square)
+            if u in VECTOR_ABS_STEPS:
+                nc.scalar.activation(square[:, second], a1, ACT.Square)
+                nc.scalar.activation(loss[:, second], b1, ACT.Abs)
+                log(whole)
+                nc.vector.scalar_tensor_tensor(loss[:, first], b0, 0.0, logarithm[:, first], ALU.max, ALU.subtract)
+                subtract(second)
+                nc.vector.scalar_tensor_tensor(difference[:, first], b0, 0.0, loss[:, first], ALU.min, ALU.subtract)
+                quantize_h(previous, whole)
+                scale(whole)
             else:
-                nc.scalar.activation(plain(sq, 0), banks[0][0], ACT.Square)
-                nc.scalar.activation(sq[:, 1], banks[1][0], ACT.Square)
-                nc.scalar.activation(part[:, 1], banks[1][1], ACT.Abs)
-                nc.scalar.activation(lg[:], sq[:], ACT.Ln, bias=1.0)
-                nc.vector.scalar_tensor_tensor(plain(part, 0), banks[0][1], 0.0, plain(lg, 0), ALU.max, ALU.subtract)
-                nc.vector.tensor_tensor(diff[:, 1], lg[:, 1], part[:, 1], ALU.subtract)
-                nc.vector.scalar_tensor_tensor(plain(diff, 0), banks[0][1], 0.0, plain(part, 0), ALU.min, ALU.subtract)
-                scale(1, False)
-                quantize_h(*pending, both)
-                scale(0, True)
-            if pending is not None and pending[0] == 1:
-                flash(pending[1], both, nc.sync)
-            pending = (a, pair, h_bf)
-            if u == 0:
-                gather_words(2, "w1_raw0")
-            if u == 1:
-                gather_words(3, "w1_raw1")
-        flash(pending[1], single[0], nc.sync)
-        quantize_h(*pending, single[1])
-        flash(pending[1], single[1], nc.scalar)
+                log(first)
+                nc.scalar.activation(loss[:, first], b0, ACT.Abs)
+                nc.scalar.activation(square[:, second], a1, ACT.Square)
+                nc.scalar.activation(loss[:, second], b1, ACT.Abs)
+                subtract(first)
+                if previous is not None:
+                    quantize_h(previous, whole)
+                scale(first)
+                if step == STEPS[-1]:
+                    quantize_h(step, first)
+                for entries in last_halves if step == STEPS[-1] else [second]:
+                    log(entries)
+                    subtract(entries)
+                    scale(entries)
+            if previous is not None and previous[0] == 1:
+                flash(previous[1], whole, nc.sync)
+            previous = step
+        flash(pair, first, nc.sync)
+        for entries in last_halves:
+            quantize_h(step, entries)
+        flash(pair, second, nc.scalar)

@@ -24,9 +24,8 @@ PAIR = 2 * BLOCK
 HALF = S // 2
 GROUP = 16
 ALIGN = 64
-STEPS = [(0, 0), (0, 1), (1, 0), (1, 1), (0, 2), (1, 2), (0, 3), (1, 3)]
-VECTOR_ABS_STEPS = range(1, 5)
-WORK_BUFS = 4
+STEPS = [(0, 0), (0, 1), (0, 2), (1, 0), (1, 1), (1, 2), (0, 3), (1, 3)]
+LAG = 2
 
 
 def tile_list_lightning_flash_layers_kernel(
@@ -35,7 +34,8 @@ def tile_list_lightning_flash_layers_kernel(
     nc = tc.nc
     with ExitStack() as ctx:
         keep = ctx.enter_context(tc.tile_pool(name="keep", bufs=1))
-        work = ctx.enter_context(tc.tile_pool(name="work", bufs=WORK_BUFS))
+        work = ctx.enter_context(tc.tile_pool(name="work", bufs=LAG))
+        ready = ctx.enter_context(tc.tile_pool(name="ready", bufs=LAG + 2))
         psum_a = ctx.enter_context(tc.psum_pool(name="psum_a", bufs=2))
         psum_b = ctx.enter_context(tc.psum_pool(name="psum_b", bufs=4))
         psum_y = ctx.enter_context(tc.psum_pool(name="psum_y", bufs=2))
@@ -88,13 +88,14 @@ def tile_list_lightning_flash_layers_kernel(
             return picked
 
         w1_bf = [held([P, PACK, P, PACK], BF16, "w1_bf%d" % a) for a in range(2)]
-        w1_q = [held([P, PASS], U32, "w1_q%d" % a) for a in range(2)]
+        w1_q = {}
         w1_s = [held([P, PASS], U8, "w1_s%d" % a) for a in range(2)]
 
         def cast_w1(copy, target, source):
             copy(target.rearrange("p t m i -> p m t i"), source.rearrange("p i (m t) -> p m t i", t=PACK))
 
-        def quantize_w1(a):
+        def quantize_w1(a, after):
+            w1_q[a] = held([P, PASS], U32, "w1_q%d" % a, after=after)
             nc.vector.quantize_mx(
                 out=w1_q[a][:].bitcast(FP8X4), scales=w1_s[a][:], in_=w1_bf[a][:].rearrange("p t m i -> p (t m i)")
             )
@@ -103,7 +104,7 @@ def tile_list_lightning_flash_layers_kernel(
         for c in range(2):
             cast_w1(nc.scalar.copy, w1_bf[0][:, :, P // 2 * c : P // 2 * (c + 1), :], w1_piece[c][:])
         v_s.append(gather_scales(1, "w1_piece0"))
-        quantize_w1(0)
+        quantize_w1(0, None)
         v_w = [gather_words(0, None)]
         w1_late = held([P, PACK, PASS], F32, "w1_late", after="w1_piece1")
         nc.sync.dma_start(w1_late[:], w1_rows[:, :, PASS:])
@@ -132,8 +133,11 @@ def tile_list_lightning_flash_layers_kernel(
             nc.sync.dma_start(
                 w3_s[r:P:32, :, :].bitcast(I32), w3_scales[:, r:16:4, :].rearrange("a q c -> q a c").bitcast(I32)
             )
-        cast_w1(nc.vector.tensor_copy, w1_bf[1][:], w1_late[:])
-        quantize_w1(1)
+
+        def round_on_gpsimd(target, source):
+            nc.gpsimd.tensor_scalar(target, source, 1.0, 0.0, ALU.mult, ALU.add)
+
+        cast_w1(round_on_gpsimd, w1_bf[1][:], w1_late[:])
 
         def products(a, pair, block):
             rhs = v_w[pair][:, BLOCK * block : BLOCK * (block + 1)].bitcast(FP8X4)
@@ -191,66 +195,55 @@ def tile_list_lightning_flash_layers_kernel(
                         start=(a == 0),
                         stop=(a == 1),
                     )
-            squared = work.tile([P, 2, width], F32, name="squared")
+            squared = held([P, 2, width], F32, "squared%d_%d" % (pair, entries.start))
             nc.scalar.activation(squared[:], bank_y[:], ACT.Square)
             j0 = PAIR * pair + entries.start
             queue.dma_start(out_rows[:, :, j0 : j0 + width], squared[:])
 
         whole = slice(0, PAIR)
         blocks = [slice(0, BLOCK), slice(BLOCK, PAIR)]
-        last_halves = [slice(BLOCK, BLOCK + BLOCK // 2), slice(BLOCK + BLOCK // 2, PAIR)]
-        previous = None
+        last = len(STEPS) - 1
+
+        def finish(u):
+            step = STEPS[u]
+            h_q[step] = held([P, PAIR], U32, "h_q%d" % u, after="logarithm%d" % min(u + LAG, last) if u + LAG <= last else None)
+            h_s[step] = ready.tile([P, PAIR], U8, name="h_s", align_bytes=ALIGN)
+            quantize_h(step, whole)
+            if step[0] == 1:
+                flash(step[1], whole, nc.sync)
+
         for u, step in enumerate(STEPS):
             a, pair = step
-            (a0, b0), (a1, b1) = [products(a, pair, block) for block in range(2)]
-            square = work.tile([P, PAIR, PACK], F32, name="square")
-            logarithm = work.tile([P, PAIR, PACK], F32, name="logarithm")
-            loss = work.tile([P, PAIR, PACK], F32, name="loss")
+            banks = [products(a, pair, block) for block in range(2)]
+            logarithm = held([P, PAIR, PACK], F32, "logarithm%d" % u)
             difference = work.tile([P, PAIR, PACK], F32, name="difference")
-            h_bf[step] = work.tile([P, PAIR, PACK], BF16, name="h_bf", align_bytes=ALIGN)
-            h_q[step] = work.tile([P, PAIR], U32, name="h_q", align_bytes=ALIGN)
-            h_s[step] = work.tile([P, PAIR], U8, name="h_s", align_bytes=ALIGN)
-
-            def log(entries):
-                nc.scalar.activation(logarithm[:, entries], square[:, entries], ACT.Ln, bias=1.0)
-
-            def subtract(entries):
-                nc.vector.tensor_tensor(difference[:, entries], logarithm[:, entries], loss[:, entries], ALU.subtract)
-
-            def scale(entries):
-                by_slot = gains[:, a : a + 1, :].broadcast_to([P, entries.stop - entries.start, PACK])
-                nc.vector.tensor_tensor(h_bf[step][:, entries], difference[:, entries], by_slot, ALU.mult)
-
-            first, second = blocks
-            nc.scalar.activation(square[:, first], a0, ACT.Square)
-            if u in VECTOR_ABS_STEPS:
-                nc.scalar.activation(square[:, second], a1, ACT.Square)
-                nc.scalar.activation(loss[:, second], b1, ACT.Abs)
-                log(whole)
-                nc.vector.scalar_tensor_tensor(loss[:, first], b0, 0.0, logarithm[:, first], ALU.max, ALU.subtract)
-                subtract(second)
-                nc.vector.scalar_tensor_tensor(difference[:, first], b0, 0.0, loss[:, first], ALU.min, ALU.subtract)
-                quantize_h(previous, whole)
-                scale(whole)
-            else:
-                log(first)
-                nc.scalar.activation(loss[:, first], b0, ACT.Abs)
-                nc.scalar.activation(square[:, second], a1, ACT.Square)
-                nc.scalar.activation(loss[:, second], b1, ACT.Abs)
-                subtract(first)
-                if previous is not None:
-                    quantize_h(previous, whole)
-                scale(first)
-                if step == STEPS[-1]:
-                    quantize_h(step, first)
-                for entries in last_halves if step == STEPS[-1] else [second]:
-                    log(entries)
-                    subtract(entries)
-                    scale(entries)
-            if previous is not None and previous[0] == 1:
-                flash(previous[1], whole, nc.sync)
-            previous = step
-        flash(pair, first, nc.sync)
-        for entries in last_halves:
-            quantize_h(step, entries)
-        flash(pair, second, nc.scalar)
+            h_bf[step] = ready.tile([P, PAIR, PACK], BF16, name="h_bf", align_bytes=ALIGN)
+            for entries, (bank_a, bank_b) in zip(blocks, banks):
+                nc.scalar.activation(logarithm[:, entries], bank_a, ACT.Square)
+            for entries in blocks if u in (0, last) else [whole]:
+                nc.scalar.activation(logarithm[:, entries], logarithm[:, entries], ACT.Ln, bias=1.0)
+            for entries, (bank_a, bank_b) in zip(blocks, banks):
+                nc.vector.scalar_tensor_tensor(
+                    difference[:, entries], bank_b, 0.0, logarithm[:, entries], ALU.max, ALU.subtract
+                )
+            for entries, (bank_a, bank_b) in zip(blocks, banks):
+                nc.vector.scalar_tensor_tensor(
+                    difference[:, entries], bank_b, 0.0, difference[:, entries], ALU.min, ALU.subtract
+                )
+            if u == LAG - 1:
+                quantize_w1(1, "logarithm%d" % u)
+            if u >= LAG:
+                finish(u - LAG)
+            if u < last:
+                by_slot = gains[:, a : a + 1, :].broadcast_to([P, PAIR, PACK])
+                nc.gpsimd.tensor_tensor(h_bf[step][:], difference[:], by_slot, ALU.mult)
+        by_slot = gains[:, a : a + 1, :].broadcast_to([P, BLOCK, PACK])
+        h_q[step] = held([P, PAIR], U32, "h_q%d" % last)
+        h_s[step] = ready.tile([P, PAIR], U8, name="h_s", align_bytes=ALIGN)
+        nc.vector.tensor_tensor(h_bf[step][:, blocks[0]], difference[:, blocks[0]], by_slot, ALU.mult)
+        finish(last - 1)
+        quantize_h(step, blocks[0])
+        nc.vector.tensor_tensor(h_bf[step][:, blocks[1]], difference[:, blocks[1]], by_slot, ALU.mult)
+        flash(pair, blocks[0], nc.sync)
+        quantize_h(step, blocks[1])
+        flash(pair, blocks[1], nc.scalar)

@@ -24,7 +24,7 @@ PAIR = 2 * BLOCK
 HALF = S // 2
 GROUP = 16
 ALIGN = 64
-STEPS = [(0, 0), (0, 1), (0, 2), (1, 0), (1, 1), (1, 2), (0, 3), (1, 3)]
+STEPS = [(a, pair) for a in range(2) for pair in range(S // PAIR)]
 LAG = 2
 
 
@@ -35,7 +35,6 @@ def tile_list_lightning_flash_layers_kernel(
     with ExitStack() as ctx:
         keep = ctx.enter_context(tc.tile_pool(name="keep", bufs=1))
         work = ctx.enter_context(tc.tile_pool(name="work", bufs=LAG))
-        ready = ctx.enter_context(tc.tile_pool(name="ready", bufs=LAG + 2))
         psum_a = ctx.enter_context(tc.psum_pool(name="psum_a", bufs=2))
         psum_b = ctx.enter_context(tc.psum_pool(name="psum_b", bufs=4))
         psum_y = ctx.enter_context(tc.psum_pool(name="psum_y", bufs=2))
@@ -46,48 +45,56 @@ def tile_list_lightning_flash_layers_kernel(
         offsets = keep.tile([P, S // GROUP], U16, name="offsets")
         nc.sync.dma_start(offsets[:], offs)
 
-        warm_in = held([P, 1], F32, "warm_in")
-        warm_out = held([P, 1], F32, "warm_out")
-        nc.gpsimd.memset(warm_in[:], 1.0)
-        nc.scalar.activation(warm_out[:], warm_in[:], ACT.Ln)
-
         tab_s = held([P, T], U8, "tab_s")
         nc.gpsimd.memset(tab_s[:].bitcast(I32), 0)
         for e in range(2):
             nc.sync.dma_start(tab_s[e:P:GROUP, :].bitcast(I32), tab_scales[0, e:16:2, :].bitcast(I32))
 
+        warm_in = held([P, 1], F32, "warm_in")
+        warm_out = held([P, 1], F32, "warm_out")
+        nc.vector.memset(warm_in[:], 1.0)
+        nc.scalar.activation(warm_out[:], warm_in[:], ACT.Ln)
+
         w1_rows = w1.rearrange("(p i) c -> p i c", i=PACK)
         w1_piece = [held([P, PACK, PASS // 2], F32, "w1_piece%d" % c) for c in range(2)]
         for c in range(2):
             nc.sync.dma_start(w1_piece[c][:], w1_rows[:, :, PASS // 2 * c : PASS // 2 * (c + 1)])
-        tab_w = held([P, T], U32, "tab_w", after="warm_in")
+        tab_w = held([P, T], U32, "tab_w")
         nc.sync.dma_start(tab_w[:].bitcast(I32), tab_words[0].rearrange("p t i -> p (t i)").bitcast(I32))
 
-        w2_in = held([P, 3 * H], U8, "w2_in", after="warm_out")
-        w2_in_w = w2_in[:, : 2 * H]
-        w2_in_s = w2_in[:, 2 * H :]
-        nc.sync.dma_start(w2_in_w.bitcast(I32), w2_words[0].bitcast(I32))
-        nc.gpsimd.memset(w2_in_s.bitcast(I32), 0)
-        for r in range(4):
-            nc.sync.dma_start(w2_in_s[r:P:32, :].bitcast(I32), w2_scales[0, r:16:4, :].bitcast(I32))
-
-        def gather_scales(half, after):
-            picked = held([P, HALF], U8, "picked_s%d" % half, after=after)
+        def gather_scales(half):
+            picked = held([P, HALF], U8, "picked_s%d" % half)
             columns = slice(HALF // GROUP * half, HALF // GROUP * (half + 1))
             nc.vector.tensor_copy(picked[:], tab_s[:].indirect(offsets[:, columns]))
-            placed = held([P, HALF], U8, "v_s%d" % half)
-            nc.vector.tensor_copy(placed[:].bitcast(I32), picked[:].bitcast(I32))
+            return picked
+
+        def move_odd_rows(placed, picked):
             for e in range(2):
                 nc.sync.dma_start(placed[2 + e : P : 32, :].bitcast(I32), picked[GROUP + e : P : 32, :].bitcast(I32))
-            return placed
 
-        def gather_words(pair, after):
-            picked = held([P, PAIR], U32, "v_w%d" % pair, after=after)
-            columns = slice(PAIR // GROUP * pair, PAIR // GROUP * (pair + 1))
+        v_s = [held([P, HALF], U8, "v_s0")]
+        nc.gpsimd.memset(v_s[0][:].bitcast(I32), 0)
+        picked_s = [gather_scales(0)]
+        for e in range(2):
+            nc.sync.dma_start(v_s[0][e:P:32, :].bitcast(I32), picked_s[0][e:P:32, :].bitcast(I32))
+        move_odd_rows(v_s[0], picked_s[0])
+        picked_s.append(gather_scales(1))
+
+        w2_in_w = held([P, 2 * H], U8, "w2_in_w")
+        nc.sync.dma_start(w2_in_w[:].bitcast(I32), w2_words[0].bitcast(I32))
+        w2_in_s = held([P, H], U8, "w2_in_s")
+        nc.gpsimd.memset(w2_in_s[:].bitcast(I32), 0)
+        for r in range(4):
+            queue = nc.gpsimd if r < 2 else nc.sync
+            queue.dma_start(w2_in_s[r:P:32, :].bitcast(I32), w2_scales[0, r:16:4, :].bitcast(I32))
+
+        def gather_words(pair, pairs, after):
+            picked = held([P, PAIR * pairs], U32, "v_w%d" % pair, after=after)
+            columns = slice(PAIR // GROUP * pair, PAIR // GROUP * (pair + pairs))
             nc.vector.tensor_copy(picked[:], tab_w[:].indirect(offsets[:, columns]))
             return picked
 
-        w1_bf = [held([P, PACK, P, PACK], BF16, "w1_bf%d" % a) for a in range(2)]
+        w1_bf = {0: held([P, PACK, P, PACK], BF16, "w1_bf0")}
         w1_q = {}
         w1_s = [held([P, PASS], U8, "w1_s%d" % a) for a in range(2)]
 
@@ -100,34 +107,34 @@ def tile_list_lightning_flash_layers_kernel(
                 out=w1_q[a][:].bitcast(FP8X4), scales=w1_s[a][:], in_=w1_bf[a][:].rearrange("p t m i -> p (t m i)")
             )
 
-        v_s = [gather_scales(0, None)]
         for c in range(2):
             cast_w1(nc.scalar.copy, w1_bf[0][:, :, P // 2 * c : P // 2 * (c + 1), :], w1_piece[c][:])
-        v_s.append(gather_scales(1, "w1_piece0"))
-        quantize_w1(0, None)
-        v_w = [gather_words(0, None)]
-        w1_late = held([P, PACK, PASS], F32, "w1_late", after="w1_piece1")
+        w1_late = held([P, PACK, PASS], F32, "w1_late", after="w1_piece0")
         nc.sync.dma_start(w1_late[:], w1_rows[:, :, PASS:])
 
-        w2_w = held([P, 2 * H], U8, "w2_w")
+        quantize_w1(0, None)
+        first = gather_words(0, 1, None)
+        v_s.append(held([P, HALF], U8, "v_s1", after="w1_bf0"))
+        nc.vector.tensor_copy(v_s[1][:].bitcast(I32), picked_s[1][:].bitcast(I32))
+        move_odd_rows(v_s[1], picked_s[1])
+        w2_mx = held([P, 3 * H], U8, "w2_mx", after="picked_s0")
+        w2_w = w2_mx[:, : 2 * H]
+        w2_s = w2_mx[:, 2 * H :]
         nc.vector.tensor_copy(
-            w2_w[:].bitcast(U16).rearrange("p (a t m) -> p a t m", a=2, t=PACK),
-            w2_in_w.bitcast(U16).rearrange("p (a m t) -> p a t m", a=2, t=PACK),
+            w2_w.bitcast(U16).rearrange("p (a t m) -> p a t m", a=2, t=PACK),
+            w2_in_w[:].bitcast(U16).rearrange("p (a m t) -> p a t m", a=2, t=PACK),
         )
-        w2_s = held([P, H], U8, "w2_s")
         nc.vector.tensor_copy(
-            w2_s[:].rearrange("p (a t m) -> p a t m", a=2, t=PACK),
-            w2_in_s.rearrange("p (a m t) -> p a t m", a=2, t=PACK),
+            w2_s.rearrange("p (a t m) -> p a t m", a=2, t=PACK),
+            w2_in_s[:].rearrange("p (a m t) -> p a t m", a=2, t=PACK),
         )
-        v_w.append(gather_words(1, "warm_out"))
-        v_w.append(gather_words(2, "picked_s0"))
-        v_w.append(gather_words(3, "w1_bf0"))
+        second = gather_words(1, 1, None)
+        rest = gather_words(2, 2, "w2_in_s")
+        v_w = [first[:], second[:], rest[:, :PAIR], rest[:, PAIR:]]
 
-        gains = held([P, 2, PACK], F32, "gains", after="tab_s")
+        gains = held([P, 2, PACK], F32, "gains", after="w2_in_w")
         nc.sync.dma_start(gains[:], gain.rearrange("(a p t) -> p a t", a=2, t=PACK))
-        w3_w = held([P, 2, N], U32, "w3_w", after="w1_piece1")
-        nc.sync.dma_start(w3_w[:].bitcast(I32), w3_words.rearrange("a p c i -> p a (c i)").bitcast(I32))
-        w3_s = held([P, 2, N], U8, "w3_s", after="w1_piece0")
+        w3_s = held([P, 2, N], U8, "w3_s", after="picked_s1")
         nc.gpsimd.memset(w3_s[:].rearrange("p a c -> p (a c)").bitcast(I32), 0)
         for r in range(4):
             nc.sync.dma_start(
@@ -137,6 +144,7 @@ def tile_list_lightning_flash_layers_kernel(
         def round_on_gpsimd(target, source):
             nc.gpsimd.tensor_scalar(target, source, 1.0, 0.0, ALU.mult, ALU.add)
 
+        w1_bf[1] = held([P, PACK, P, PACK], BF16, "w1_bf1", after="tab_w")
         cast_w1(round_on_gpsimd, w1_bf[1][:], w1_late[:])
 
         def products(a, pair, block):
@@ -181,9 +189,9 @@ def tile_list_lightning_flash_layers_kernel(
 
         out_rows = out.rearrange("(c p) j -> p c j", p=P)
 
-        def flash(pair, entries, queue):
+        def flash(pair, entries, queue, pool, tag):
             width = entries.stop - entries.start
-            bank_y = psum_y.tile([P, 2, width], F32, name="bank_y")
+            bank_y = pool.tile([P, 2, width], F32, name="bank_y", tag=tag)
             for c in range(2):
                 for a in range(2):
                     nc.tensor.matmul_mx(
@@ -207,20 +215,20 @@ def tile_list_lightning_flash_layers_kernel(
         def finish(u):
             step = STEPS[u]
             h_q[step] = held([P, PAIR], U32, "h_q%d" % u, after="logarithm%d" % min(u + LAG, last) if u + LAG <= last else None)
-            h_s[step] = ready.tile([P, PAIR], U8, name="h_s", align_bytes=ALIGN)
+            h_s[step] = held([P, PAIR], U8, "h_s%d%d" % step)
             quantize_h(step, whole)
             if step[0] == 1:
-                flash(step[1], whole, nc.sync)
+                flash(step[1], whole, nc.sync, psum_y, "bank_y")
 
         for u, step in enumerate(STEPS):
             a, pair = step
             banks = [products(a, pair, block) for block in range(2)]
             logarithm = held([P, PAIR, PACK], F32, "logarithm%d" % u)
             difference = work.tile([P, PAIR, PACK], F32, name="difference")
-            h_bf[step] = ready.tile([P, PAIR, PACK], BF16, name="h_bf", align_bytes=ALIGN)
+            h_bf[step] = held([P, PAIR, PACK], BF16, "h_bf%d" % u, after="h_bf%d" % (u - 1) if u == last else None)
             for entries, (bank_a, bank_b) in zip(blocks, banks):
                 nc.scalar.activation(logarithm[:, entries], bank_a, ACT.Square)
-            for entries in blocks if u in (0, last) else [whole]:
+            for entries in blocks:
                 nc.scalar.activation(logarithm[:, entries], logarithm[:, entries], ACT.Ln, bias=1.0)
             for entries, (bank_a, bank_b) in zip(blocks, banks):
                 nc.vector.scalar_tensor_tensor(
@@ -230,6 +238,9 @@ def tile_list_lightning_flash_layers_kernel(
                 nc.vector.scalar_tensor_tensor(
                     difference[:, entries], bank_b, 0.0, difference[:, entries], ALU.min, ALU.subtract
                 )
+            if u == 0:
+                w3_w = held([P, 2, N], U32, "w3_w", after="logarithm0")
+                nc.sync.dma_start(w3_w[:].bitcast(I32), w3_words.rearrange("a p c i -> p a (c i)").bitcast(I32))
             if u == LAG - 1:
                 quantize_w1(1, "logarithm%d" % u)
             if u >= LAG:
@@ -239,11 +250,11 @@ def tile_list_lightning_flash_layers_kernel(
                 nc.gpsimd.tensor_tensor(h_bf[step][:], difference[:], by_slot, ALU.mult)
         by_slot = gains[:, a : a + 1, :].broadcast_to([P, BLOCK, PACK])
         h_q[step] = held([P, PAIR], U32, "h_q%d" % last)
-        h_s[step] = ready.tile([P, PAIR], U8, name="h_s", align_bytes=ALIGN)
-        nc.vector.tensor_tensor(h_bf[step][:, blocks[0]], difference[:, blocks[0]], by_slot, ALU.mult)
+        h_s[step] = held([P, PAIR], U8, "h_s%d%d" % step)
         finish(last - 1)
-        quantize_h(step, blocks[0])
-        nc.vector.tensor_tensor(h_bf[step][:, blocks[1]], difference[:, blocks[1]], by_slot, ALU.mult)
-        flash(pair, blocks[0], nc.sync)
-        quantize_h(step, blocks[1])
-        flash(pair, blocks[1], nc.scalar)
+        for entries in blocks:
+            nc.vector.tensor_tensor(h_bf[step][:, entries], difference[:, entries], by_slot, ALU.mult)
+        for entries in blocks:
+            quantize_h(step, entries)
+        flash(pair, blocks[0], nc.sync, psum_a, "bank_a")
+        flash(pair, blocks[1], nc.scalar, psum_a, "bank_a")

@@ -47,8 +47,7 @@ def tile_list_lightning_flash_layers_kernel(
 
         tab_s = held([P, T], U8, "tab_s")
         nc.gpsimd.memset(tab_s[:].bitcast(I32), 0)
-        for e in range(2):
-            nc.sync.dma_start(tab_s[e:P:GROUP, :].bitcast(I32), tab_scales[0, e:16:2, :].bitcast(I32))
+        nc.sync.dma_start(tab_s[0:P:8, :].bitcast(I32), tab_scales[0].bitcast(I32))
 
         warm_in = held([P, 1], F32, "warm_in")
         warm_out = held([P, 1], F32, "warm_out")
@@ -68,16 +67,14 @@ def tile_list_lightning_flash_layers_kernel(
             nc.vector.tensor_copy(picked[:], tab_s[:].indirect(offsets[:, columns]))
             return picked
 
-        def move_odd_rows(placed, picked):
-            for e in range(2):
-                nc.sync.dma_start(placed[2 + e : P : 32, :].bitcast(I32), picked[GROUP + e : P : 32, :].bitcast(I32))
+        def move_rows(placed, picked, rows):
+            for r in rows:
+                nc.sync.dma_start(placed[r:P:32, :].bitcast(I32), picked[8 * r : P : 32, :].bitcast(I32))
 
         v_s = [held([P, HALF], U8, "v_s0")]
         nc.gpsimd.memset(v_s[0][:].bitcast(I32), 0)
         picked_s = [gather_scales(0)]
-        for e in range(2):
-            nc.sync.dma_start(v_s[0][e:P:32, :].bitcast(I32), picked_s[0][e:P:32, :].bitcast(I32))
-        move_odd_rows(v_s[0], picked_s[0])
+        move_rows(v_s[0], picked_s[0], range(4))
         picked_s.append(gather_scales(1))
 
         w2_in_w = held([P, 2 * H], U8, "w2_in_w")
@@ -114,9 +111,10 @@ def tile_list_lightning_flash_layers_kernel(
 
         quantize_w1(0, None)
         first = gather_words(0, 1, None)
+        second = gather_words(1, 1, None)
         v_s.append(held([P, HALF], U8, "v_s1", after="w1_bf0"))
         nc.vector.tensor_copy(v_s[1][:].bitcast(I32), picked_s[1][:].bitcast(I32))
-        move_odd_rows(v_s[1], picked_s[1])
+        move_rows(v_s[1], picked_s[1], range(1, 4))
         w2_mx = held([P, 3 * H], U8, "w2_mx", after="picked_s0")
         w2_w = w2_mx[:, : 2 * H]
         w2_s = w2_mx[:, 2 * H :]
@@ -128,11 +126,10 @@ def tile_list_lightning_flash_layers_kernel(
             w2_s.rearrange("p (a t m) -> p a t m", a=2, t=PACK),
             w2_in_s[:].rearrange("p (a m t) -> p a t m", a=2, t=PACK),
         )
-        second = gather_words(1, 1, None)
         rest = gather_words(2, 2, "w2_in_s")
         v_w = [first[:], second[:], rest[:, :PAIR], rest[:, PAIR:]]
 
-        gains = held([P, 2, PACK], F32, "gains", after="w2_in_w")
+        gains = held([P, 2, PACK], F32, "gains", after="w1_piece1")
         nc.sync.dma_start(gains[:], gain.rearrange("(a p t) -> p a t", a=2, t=PACK))
         w3_s = held([P, 2, N], U8, "w3_s", after="picked_s1")
         nc.gpsimd.memset(w3_s[:].rearrange("p a c -> p (a c)").bitcast(I32), 0)
@@ -144,7 +141,7 @@ def tile_list_lightning_flash_layers_kernel(
         def round_on_gpsimd(target, source):
             nc.gpsimd.tensor_scalar(target, source, 1.0, 0.0, ALU.mult, ALU.add)
 
-        w1_bf[1] = held([P, PACK, P, PACK], BF16, "w1_bf1", after="tab_w")
+        w1_bf[1] = held([P, PACK, P, PACK], BF16, "w1_bf1", after="w2_in_w")
         cast_w1(round_on_gpsimd, w1_bf[1][:], w1_late[:])
 
         def products(a, pair, block):
@@ -212,31 +209,38 @@ def tile_list_lightning_flash_layers_kernel(
         blocks = [slice(0, BLOCK), slice(BLOCK, PAIR)]
         last = len(STEPS) - 1
 
-        def finish(u):
+        def finish(u, after):
             step = STEPS[u]
-            h_q[step] = held([P, PAIR], U32, "h_q%d" % u, after="logarithm%d" % min(u + LAG, last) if u + LAG <= last else None)
-            h_s[step] = held([P, PAIR], U8, "h_s%d%d" % step)
+            h_q[step] = held([P, PAIR], U32, "h_q%d" % u, after=after)
+            h_s[step] = held([P, PAIR], U8, "h_s%d" % u)
             quantize_h(step, whole)
             if step[0] == 1:
                 flash(step[1], whole, nc.sync, psum_y, "bank_y")
 
+        def apply_gain(engine, u, entries):
+            a = STEPS[u][0]
+            by_slot = gains[:, a : a + 1, :].broadcast_to([P, entries.stop - entries.start, PACK])
+            engine.tensor_tensor(h_bf[STEPS[u]][:, entries], difference[u][:, entries], by_slot, ALU.mult)
+
+        difference = {}
         for u, step in enumerate(STEPS):
             a, pair = step
             banks = [products(a, pair, block) for block in range(2)]
             logarithm = held([P, PAIR, PACK], F32, "logarithm%d" % u)
-            difference = work.tile([P, PAIR, PACK], F32, name="difference")
-            h_bf[step] = held([P, PAIR, PACK], BF16, "h_bf%d" % u, after="h_bf%d" % (u - 1) if u == last else None)
             for entries, (bank_a, bank_b) in zip(blocks, banks):
                 nc.scalar.activation(logarithm[:, entries], bank_a, ACT.Square)
             for entries in blocks:
                 nc.scalar.activation(logarithm[:, entries], logarithm[:, entries], ACT.Ln, bias=1.0)
+            if u == last:
+                break
+            difference[u] = work.tile([P, PAIR, PACK], F32, name="difference")
             for entries, (bank_a, bank_b) in zip(blocks, banks):
                 nc.vector.scalar_tensor_tensor(
-                    difference[:, entries], bank_b, 0.0, logarithm[:, entries], ALU.max, ALU.subtract
+                    difference[u][:, entries], bank_b, 0.0, logarithm[:, entries], ALU.max, ALU.subtract
                 )
             for entries, (bank_a, bank_b) in zip(blocks, banks):
                 nc.vector.scalar_tensor_tensor(
-                    difference[:, entries], bank_b, 0.0, difference[:, entries], ALU.min, ALU.subtract
+                    difference[u][:, entries], bank_b, 0.0, difference[u][:, entries], ALU.min, ALU.subtract
                 )
             if u == 0:
                 w3_w = held([P, 2, N], U32, "w3_w", after="logarithm0")
@@ -244,16 +248,27 @@ def tile_list_lightning_flash_layers_kernel(
             if u == LAG - 1:
                 quantize_w1(1, "logarithm%d" % u)
             if u >= LAG:
-                finish(u - LAG)
-            if u < last:
-                by_slot = gains[:, a : a + 1, :].broadcast_to([P, PAIR, PACK])
-                nc.gpsimd.tensor_tensor(h_bf[step][:], difference[:], by_slot, ALU.mult)
-        by_slot = gains[:, a : a + 1, :].broadcast_to([P, BLOCK, PACK])
+                finish(u - LAG, "logarithm%d" % u)
+            if u < last - 1:
+                h_bf[step] = held([P, PAIR, PACK], BF16, "h_bf%d" % u)
+                for entries in blocks if u == 0 else [whole]:
+                    apply_gain(nc.gpsimd, u, entries)
+
+        loss = held([P, PAIR, PACK], F32, "loss")
+        for entries, (bank_a, bank_b) in zip(blocks, banks):
+            nc.scalar.activation(loss[:, entries], bank_b, ACT.Abs)
+        finish(last - 2, None)
+        h_bf[STEPS[last - 1]] = held([P, PAIR, PACK], BF16, "h_bf%d" % (last - 1))
+        apply_gain(nc.vector, last - 1, whole)
+        difference[last] = held([P, PAIR, PACK], F32, "difference_last", after="h_bf%d" % (last - 3))
+        h_bf[step] = held([P, PAIR, PACK], BF16, "h_bf%d" % last)
+        nc.vector.tensor_tensor(difference[last][:, blocks[0]], logarithm[:, blocks[0]], loss[:, blocks[0]], ALU.subtract)
+        finish(last - 1, None)
+        nc.vector.tensor_tensor(difference[last][:, blocks[1]], logarithm[:, blocks[1]], loss[:, blocks[1]], ALU.subtract)
         h_q[step] = held([P, PAIR], U32, "h_q%d" % last)
-        h_s[step] = held([P, PAIR], U8, "h_s%d%d" % step)
-        finish(last - 1)
+        h_s[step] = held([P, PAIR], U8, "h_s%d" % last)
         for entries in blocks:
-            nc.vector.tensor_tensor(h_bf[step][:, entries], difference[:, entries], by_slot, ALU.mult)
+            apply_gain(nc.vector, last, entries)
         for entries in blocks:
             quantize_h(step, entries)
         flash(pair, blocks[0], nc.sync, psum_a, "bank_a")

@@ -171,7 +171,7 @@ def tile_list_lightning_flash_layers_kernel(
                     start=True,
                     stop=True,
                 )
-            return bank_a[:].rearrange("p t j -> p j t"), bank_b[:].rearrange("p t j -> p j t")
+            return bank_a[:], bank_b[:]
 
         h_bf = {}
         h_q = {}
@@ -189,16 +189,16 @@ def tile_list_lightning_flash_layers_kernel(
         def flash(pair, entries, queue, pool, tag):
             width = entries.stop - entries.start
             bank_y = pool.tile([P, 2, width], F32, name="bank_y", tag=tag)
-            for c in range(2):
-                for a in range(2):
+            for a in range(2):
+                for c in range(2):
                     nc.tensor.matmul_mx(
                         out=bank_y[:, c, :],
                         lhsT=w3_w[:, a, P * c : P * (c + 1)].bitcast(FP8X4),
                         lhsT_scale=w3_s[:, a, P * c : P * (c + 1)],
                         rhs=h_q[(a, pair)][:, entries].bitcast(FP8X4),
                         rhs_scale=h_s[(a, pair)][:, entries],
-                        start=(a == 0),
-                        stop=(a == 1),
+                        start=(a, c) == (0, 0),
+                        stop=(a, c) == (1, 1),
                     )
             squared = held([P, 2, width], F32, "squared%d_%d" % (pair, entries.start))
             nc.scalar.activation(squared[:], bank_y[:], ACT.Square)
@@ -220,27 +220,34 @@ def tile_list_lightning_flash_layers_kernel(
         def apply_gain(engine, u, entries):
             a = STEPS[u][0]
             by_slot = gains[:, a : a + 1, :].broadcast_to([P, entries.stop - entries.start, PACK])
-            engine.tensor_tensor(h_bf[STEPS[u]][:, entries], difference[u][:, entries], by_slot, ALU.mult)
+            flat = difference[u][:].rearrange("p b j t -> p (b j) t")
+            engine.tensor_tensor(h_bf[STEPS[u]][:, entries], flat[:, entries], by_slot, ALU.mult)
 
         difference = {}
         for u, step in enumerate(STEPS):
             a, pair = step
             banks = [products(a, pair, block) for block in range(2)]
-            logarithm = held([P, PAIR, PACK], F32, "logarithm%d" % u)
-            for entries, (bank_a, bank_b) in zip(blocks, banks):
-                nc.scalar.activation(logarithm[:, entries], bank_a, ACT.Square)
-            for entries in blocks:
-                nc.scalar.activation(logarithm[:, entries], logarithm[:, entries], ACT.Ln, bias=1.0)
+            for block in range(2):
+                if (u, block) != (last - 1, 0):
+                    banks[block] = [bank.rearrange("p t j -> p j t") for bank in banks[block]]
+                else:
+                    banks[block] = [bank.rearrange("p t (j e) -> p (t j) e", e=PACK) for bank in banks[block]]
+            shape = [P, 2, BLOCK, PACK]
+            logarithm = held(shape, F32, "logarithm%d" % u)
+            for block in range(2):
+                nc.scalar.activation(logarithm[:, block], banks[block][0], ACT.Square)
+            for block in range(2):
+                nc.scalar.activation(logarithm[:, block], logarithm[:, block], ACT.Ln, bias=1.0)
             if u == last:
                 break
-            difference[u] = work.tile([P, PAIR, PACK], F32, name="difference")
-            for entries, (bank_a, bank_b) in zip(blocks, banks):
+            difference[u] = work.tile(shape, F32, name="difference")
+            for block in range(2):
                 nc.vector.scalar_tensor_tensor(
-                    difference[u][:, entries], bank_b, 0.0, logarithm[:, entries], ALU.max, ALU.subtract
+                    difference[u][:, block], banks[block][1], 0.0, logarithm[:, block], ALU.max, ALU.subtract
                 )
-            for entries, (bank_a, bank_b) in zip(blocks, banks):
+            for block in range(2):
                 nc.vector.scalar_tensor_tensor(
-                    difference[u][:, entries], bank_b, 0.0, difference[u][:, entries], ALU.min, ALU.subtract
+                    difference[u][:, block], banks[block][1], 0.0, difference[u][:, block], ALU.min, ALU.subtract
                 )
             if u == 0:
                 w3_w = held([P, 2, N], U32, "w3_w", after="logarithm0")
@@ -254,17 +261,22 @@ def tile_list_lightning_flash_layers_kernel(
                 for entries in blocks if u == 0 else [whole]:
                     apply_gain(nc.gpsimd, u, entries)
 
-        loss = held([P, PAIR, PACK], F32, "loss")
-        for entries, (bank_a, bank_b) in zip(blocks, banks):
-            nc.scalar.activation(loss[:, entries], bank_b, ACT.Abs)
-        finish(last - 2, None)
+        loss = held([P, 2, BLOCK, PACK], F32, "loss")
+        for block in range(2):
+            nc.scalar.activation(loss[:, block], banks[block][1], ACT.Abs)
+        by_slot = difference[last - 1][:, 0].rearrange("p (t j) e -> p t (j e)", t=PACK)
+        by_slot_bf = held([P, PACK, BLOCK], BF16, "by_slot_bf")
+        for t in range(PACK):
+            nc.scalar.activation(by_slot_bf[:, t, :], by_slot[:, t, :], ACT.Copy, scale=gains[:, a, t : t + 1])
         h_bf[STEPS[last - 1]] = held([P, PAIR, PACK], BF16, "h_bf%d" % (last - 1))
-        apply_gain(nc.vector, last - 1, whole)
-        difference[last] = held([P, PAIR, PACK], F32, "difference_last", after="h_bf%d" % (last - 3))
+        nc.scalar.copy(h_bf[STEPS[last - 1]][:, blocks[0]], by_slot_bf[:].rearrange("p t j -> p j t"))
+        finish(last - 2, None)
+        apply_gain(nc.vector, last - 1, blocks[1])
+        difference[last] = held([P, 2, BLOCK, PACK], F32, "difference_last", after="h_bf%d" % (last - 3))
         h_bf[step] = held([P, PAIR, PACK], BF16, "h_bf%d" % last)
-        nc.vector.tensor_tensor(difference[last][:, blocks[0]], logarithm[:, blocks[0]], loss[:, blocks[0]], ALU.subtract)
+        for block in range(2):
+            nc.vector.tensor_tensor(difference[last][:, block], logarithm[:, block], loss[:, block], ALU.subtract)
         finish(last - 1, None)
-        nc.vector.tensor_tensor(difference[last][:, blocks[1]], logarithm[:, blocks[1]], loss[:, blocks[1]], ALU.subtract)
         h_q[step] = held([P, PAIR], U32, "h_q%d" % last)
         h_s[step] = held([P, PAIR], U8, "h_s%d" % last)
         for entries in blocks:

@@ -82,13 +82,12 @@ def tile_list_lightning_flash_layers_kernel(
         w2_in_s = held([P, H], U8, "w2_in_s")
         nc.gpsimd.memset(w2_in_s[:].bitcast(I32), 0)
         for r in range(4):
-            queue = nc.gpsimd if r < 2 else nc.sync
+            queue = nc.gpsimd if r < 3 else nc.sync
             queue.dma_start(w2_in_s[r:P:32, :].bitcast(I32), w2_scales[0, r:16:4, :].bitcast(I32))
 
-        def gather_words(pair, pairs, after):
-            picked = held([P, PAIR * pairs], U32, "v_w%d" % pair, after=after)
-            columns = slice(PAIR // GROUP * pair, PAIR // GROUP * (pair + pairs))
-            nc.vector.tensor_copy(picked[:], tab_w[:].indirect(offsets[:, columns]))
+        def gather_words(pair, picked):
+            columns = slice(PAIR // GROUP * pair, PAIR // GROUP * (pair + 1))
+            nc.vector.tensor_copy(picked, tab_w[:].indirect(offsets[:, columns]))
             return picked
 
         w1_bf = {0: held([P, PACK, P, PACK], BF16, "w1_bf0")}
@@ -110,8 +109,8 @@ def tile_list_lightning_flash_layers_kernel(
         nc.sync.dma_start(w1_late[:], w1_rows[:, :, PASS:])
 
         quantize_w1(0, None)
-        first = gather_words(0, 1, None)
-        second = gather_words(1, 1, None)
+        first = gather_words(0, held([P, PAIR], U32, "v_w0")[:])
+        second = gather_words(1, held([P, PAIR], U32, "v_w1")[:])
         v_s.append(held([P, HALF], U8, "v_s1", after="w1_bf0"))
         nc.vector.tensor_copy(v_s[1][:].bitcast(I32), picked_s[1][:].bitcast(I32))
         move_rows(v_s[1], picked_s[1], range(1, 4))
@@ -126,8 +125,8 @@ def tile_list_lightning_flash_layers_kernel(
             w2_s.rearrange("p (a t m) -> p a t m", a=2, t=PACK),
             w2_in_s[:].rearrange("p (a m t) -> p a t m", a=2, t=PACK),
         )
-        rest = gather_words(2, 2, "w2_in_s")
-        v_w = [first[:], second[:], rest[:, :PAIR], rest[:, PAIR:]]
+        rest = held([P, 2, PAIR], U32, "v_w_rest", after="w2_in_w")
+        v_w = [first, second] + [gather_words(2 + k, rest[:, k, :]) for k in range(2)]
 
         gains = held([P, 2, PACK], F32, "gains", after="w1_piece1")
         nc.sync.dma_start(gains[:], gain.rearrange("(a p t) -> p a t", a=2, t=PACK))
@@ -141,7 +140,7 @@ def tile_list_lightning_flash_layers_kernel(
         def round_on_gpsimd(target, source):
             nc.gpsimd.tensor_scalar(target, source, 1.0, 0.0, ALU.mult, ALU.add)
 
-        w1_bf[1] = held([P, PACK, P, PACK], BF16, "w1_bf1", after="w2_in_w")
+        w1_bf[1] = held([P, PACK, P, PACK], BF16, "w1_bf1", after="w2_in_s")
         cast_w1(round_on_gpsimd, w1_bf[1][:], w1_late[:])
 
         def products(a, pair, block):

@@ -21,7 +21,7 @@ PACK = 4
 PASS = P * PACK
 BLOCK = 128
 PAIR = 2 * BLOCK
-HALF = S // 2
+PIECE = 256
 GROUP = 16
 ALIGN = 64
 STEPS = [(a, pair) for a in range(2) for pair in range(S // PAIR)]
@@ -43,6 +43,14 @@ def tile_list_lightning_flash_layers_kernel(
             return keep.tile(shape, dtype, name=name, tag=after or name, align_bytes=ALIGN)
 
         offsets = keep.tile([P, S // GROUP], U16, name="offsets")
+        w1_rows = w1.rearrange("(p i) c -> p i c", i=PACK)
+        w1_piece = {}
+
+        def load_w1(c, after=None):
+            w1_piece[c] = held([P, PACK, PIECE], F32, "w1_piece%d" % c, after=after)
+            nc.sync.dma_start(w1_piece[c][:], w1_rows[:, :, PIECE * c : PIECE * (c + 1)])
+
+        load_w1(0)
         nc.sync.dma_start(offsets[:], offs)
 
         tab_s = held([P, T], U8, "tab_s")
@@ -54,30 +62,27 @@ def tile_list_lightning_flash_layers_kernel(
         nc.vector.memset(warm_in[:], 1.0)
         nc.scalar.activation(warm_out[:], warm_in[:], ACT.Ln)
 
-        w1_rows = w1.rearrange("(p i) c -> p i c", i=PACK)
-        w1_piece = [held([P, PACK, PASS // 2], F32, "w1_piece%d" % c) for c in range(2)]
-        for c in range(2):
-            nc.sync.dma_start(w1_piece[c][:], w1_rows[:, :, PASS // 2 * c : PASS // 2 * (c + 1)])
+        load_w1(1)
         tab_w = held([P, T], U32, "tab_w")
         nc.sync.dma_start(tab_w[:].bitcast(I32), tab_words[0].rearrange("p t i -> p (t i)").bitcast(I32))
 
-        def gather_scales(half):
-            picked = held([P, HALF], U8, "picked_s%d" % half)
-            columns = slice(HALF // GROUP * half, HALF // GROUP * (half + 1))
-            nc.vector.tensor_copy(picked[:], tab_s[:].indirect(offsets[:, columns]))
+        load_w1(2)
+
+        def gather_scales(name, start, stop):
+            picked = held([P, stop - start], U8, name)
+            nc.vector.tensor_copy(picked[:], tab_s[:].indirect(offsets[:, start // GROUP : stop // GROUP]))
             return picked
 
         def move_rows(placed, picked, rows):
             for r in rows:
                 nc.sync.dma_start(placed[r:P:32, :].bitcast(I32), picked[8 * r : P : 32, :].bitcast(I32))
 
-        v_s = [held([P, HALF], U8, "v_s0")]
-        nc.gpsimd.memset(v_s[0][:].bitcast(I32), 0)
-        picked_s = [gather_scales(0)]
-        move_rows(v_s[0], picked_s[0], range(4))
-        picked_s.append(gather_scales(1))
+        first_s = held([P, PAIR], U8, "first_s")
+        nc.gpsimd.memset(first_s[:].bitcast(I32), 0)
+        move_rows(first_s, gather_scales("picked_first", 0, PAIR), range(4))
+        picked_rest = gather_scales("picked_rest", PAIR, S)
 
-        w2_in_w = held([P, 2 * H], U8, "w2_in_w")
+        w2_in_w = held([P, 2 * H], U8, "w2_in_w", after="w1_piece1")
         nc.sync.dma_start(w2_in_w[:].bitcast(I32), w2_words[0].bitcast(I32))
         w2_in_s = held([P, H], U8, "w2_in_s")
         nc.gpsimd.memset(w2_in_s[:].bitcast(I32), 0)
@@ -90,12 +95,17 @@ def tile_list_lightning_flash_layers_kernel(
             nc.vector.tensor_copy(picked, tab_w[:].indirect(offsets[:, columns]))
             return picked
 
-        w1_bf = {0: held([P, PACK, P, PACK], BF16, "w1_bf0")}
+        w1_bf = [held([P, PACK, P, PACK], BF16, "w1_bf%d" % a) for a in range(2)]
         w1_q = {}
         w1_s = [held([P, PASS], U8, "w1_s%d" % a) for a in range(2)]
 
-        def cast_w1(copy, target, source):
-            copy(target.rearrange("p t m i -> p m t i"), source.rearrange("p i (m t) -> p m t i", t=PACK))
+        def round_w1(copy, c):
+            a, half = divmod(c, 2)
+            target = w1_bf[a][:, :, P // 2 * half : P // 2 * (half + 1), :]
+            copy(target.rearrange("p t m i -> p m t i"), w1_piece[c][:].rearrange("p i (m t) -> p m t i", t=PACK))
+
+        def round_on_gpsimd(target, source):
+            nc.gpsimd.tensor_scalar(target, source, 1.0, 0.0, ALU.mult, ALU.add)
 
         def quantize_w1(a, after):
             w1_q[a] = held([P, PASS], U32, "w1_q%d" % a, after=after)
@@ -103,50 +113,43 @@ def tile_list_lightning_flash_layers_kernel(
                 out=w1_q[a][:].bitcast(FP8X4), scales=w1_s[a][:], in_=w1_bf[a][:].rearrange("p t m i -> p (t m i)")
             )
 
-        for c in range(2):
-            cast_w1(nc.scalar.copy, w1_bf[0][:, :, P // 2 * c : P // 2 * (c + 1), :], w1_piece[c][:])
-        w1_late = held([P, PACK, PASS], F32, "w1_late", after="w1_piece0")
-        nc.sync.dma_start(w1_late[:], w1_rows[:, :, PASS:])
-
+        for c in range(3):
+            round_w1(nc.scalar.copy, c)
         quantize_w1(0, None)
-        first = gather_words(0, held([P, PAIR], U32, "v_w0")[:])
-        second = gather_words(1, held([P, PAIR], U32, "v_w1")[:])
-        v_s.append(held([P, HALF], U8, "v_s1", after="w1_bf0"))
-        nc.vector.tensor_copy(v_s[1][:].bitcast(I32), picked_s[1][:].bitcast(I32))
-        move_rows(v_s[1], picked_s[1], range(1, 4))
-        w2_mx = held([P, 3 * H], U8, "w2_mx", after="picked_s0")
-        w2_w = w2_mx[:, : 2 * H]
-        w2_s = w2_mx[:, 2 * H :]
-        nc.vector.tensor_copy(
-            w2_w.bitcast(U16).rearrange("p (a t m) -> p a t m", a=2, t=PACK),
-            w2_in_w[:].bitcast(U16).rearrange("p (a m t) -> p a t m", a=2, t=PACK),
-        )
-        nc.vector.tensor_copy(
-            w2_s.rearrange("p (a t m) -> p a t m", a=2, t=PACK),
-            w2_in_s[:].rearrange("p (a m t) -> p a t m", a=2, t=PACK),
-        )
-        rest = held([P, 2, PAIR], U32, "v_w_rest", after="w2_in_w")
-        v_w = [first, second] + [gather_words(2 + k, rest[:, k, :]) for k in range(2)]
+        first_w = gather_words(0, held([P, PAIR], U32, "v_w0")[:])
+        rest_s = held([P, S - PAIR], U8, "rest_s", after="tab_s")
+        nc.vector.tensor_copy(rest_s[:].bitcast(I32), picked_rest[:].bitcast(I32))
+        move_rows(rest_s, picked_rest, range(1, 4))
+        second_w = gather_words(1, held([P, PAIR], U32, "v_w1")[:])
+        w2_s = held([P, H], U8, "w2_s", after="w1_bf0")
+        w2_w = held([P, 2 * H], U8, "w2_w")
+        for a in range(2):
+            nc.vector.tensor_copy(
+                w2_s[:, PASS * a : PASS * (a + 1)].rearrange("p (t m) -> p t m", t=PACK),
+                w2_in_s[:, PASS * a : PASS * (a + 1)].rearrange("p (m t) -> p t m", t=PACK),
+            )
+            nc.vector.tensor_copy(
+                w2_w[:].bitcast(U16)[:, PASS * a : PASS * (a + 1)].rearrange("p (t m) -> p t m", t=PACK),
+                w2_in_w[:].bitcast(U16)[:, PASS * a : PASS * (a + 1)].rearrange("p (m t) -> p t m", t=PACK),
+            )
+        rest_w = held([P, 2, PAIR], U32, "v_w_rest", after="w1_piece1")
+        v_w = [first_w, second_w] + [gather_words(2 + k, rest_w[:, k, :]) for k in range(2)]
+        v_s = [first_s[:]] + [rest_s[:, PAIR * k : PAIR * (k + 1)] for k in range(3)]
 
-        gains = held([P, 2, PACK], F32, "gains", after="w1_piece1")
+        load_w1(3, "picked_first")
+        round_w1(round_on_gpsimd, 3)
+        gains = held([P, 2, PACK], F32, "gains", after="w1_piece2")
         nc.sync.dma_start(gains[:], gain.rearrange("(a p t) -> p a t", a=2, t=PACK))
-        w3_s = held([P, 2, N], U8, "w3_s", after="picked_s1")
-        nc.gpsimd.memset(w3_s[:].rearrange("p a c -> p (a c)").bitcast(I32), 0)
+        w3_s = held([P, 2, N], U8, "w3_s", after="picked_rest")
+        nc.vector.memset(w3_s[:].rearrange("p a c -> p (a c)").bitcast(I32), 0)
         for r in range(4):
             nc.sync.dma_start(
                 w3_s[r:P:32, :, :].bitcast(I32), w3_scales[:, r:16:4, :].rearrange("a q c -> q a c").bitcast(I32)
             )
 
-        def round_on_gpsimd(target, source):
-            nc.gpsimd.tensor_scalar(target, source, 1.0, 0.0, ALU.mult, ALU.add)
-
-        w1_bf[1] = held([P, PACK, P, PACK], BF16, "w1_bf1", after="w2_in_s")
-        cast_w1(round_on_gpsimd, w1_bf[1][:], w1_late[:])
-
         def products(a, pair, block):
             rhs = v_w[pair][:, BLOCK * block : BLOCK * (block + 1)].bitcast(FP8X4)
-            half, j0 = divmod(PAIR * pair + BLOCK * block, HALF)
-            rhs_scale = v_s[half][:, j0 : j0 + BLOCK]
+            rhs_scale = v_s[pair][:, BLOCK * block : BLOCK * (block + 1)]
             bank_a = psum_a.tile([P, PACK, BLOCK], F32, name="bank_a")
             bank_b = psum_b.tile([P, PACK, BLOCK], F32, name="bank_b")
             for t in range(PACK):

@@ -90,6 +90,10 @@ def tile_list_lightning_flash_layers_kernel(
             queue = nc.gpsimd if r < 3 else nc.sync
             queue.dma_start(w2_in_s[r:P:32, :].bitcast(I32), w2_scales[0, r:16:4, :].bitcast(I32))
 
+        rest_s = held([P, S - PAIR], U8, "rest_s")
+        nc.gpsimd.memset(rest_s[:].bitcast(I32), 0)
+        move_rows(rest_s, picked_rest, range(4))
+
         def gather_words(pair, picked):
             columns = slice(PAIR // GROUP * pair, PAIR // GROUP * (pair + 1))
             nc.vector.tensor_copy(picked, tab_w[:].indirect(offsets[:, columns]))
@@ -117,9 +121,6 @@ def tile_list_lightning_flash_layers_kernel(
             round_w1(nc.scalar.copy, c)
         quantize_w1(0, None)
         first_w = gather_words(0, held([P, PAIR], U32, "v_w0")[:])
-        rest_s = held([P, S - PAIR], U8, "rest_s", after="tab_s")
-        nc.vector.tensor_copy(rest_s[:].bitcast(I32), picked_rest[:].bitcast(I32))
-        move_rows(rest_s, picked_rest, range(1, 4))
         second_w = gather_words(1, held([P, PAIR], U32, "v_w1")[:])
         w2_s = held([P, H], U8, "w2_s", after="w1_bf0")
         w2_w = held([P, 2 * H], U8, "w2_w")
@@ -132,16 +133,16 @@ def tile_list_lightning_flash_layers_kernel(
                 w2_w[:].bitcast(U16)[:, PASS * a : PASS * (a + 1)].rearrange("p (t m) -> p t m", t=PACK),
                 w2_in_w[:].bitcast(U16)[:, PASS * a : PASS * (a + 1)].rearrange("p (m t) -> p t m", t=PACK),
             )
-        rest_w = held([P, 2, PAIR], U32, "v_w_rest", after="w1_piece1")
-        v_w = [first_w, second_w] + [gather_words(2 + k, rest_w[:, k, :]) for k in range(2)]
+        rest_w = held([P, 2 * PAIR], U32, "v_w_rest", after="w1_piece1")
+        nc.vector.tensor_copy(rest_w[:], tab_w[:].indirect(offsets[:, 2 * PAIR // GROUP : S // GROUP]))
+        v_w = [first_w, second_w] + [rest_w[:, PAIR * k : PAIR * (k + 1)] for k in range(2)]
         v_s = [first_s[:]] + [rest_s[:, PAIR * k : PAIR * (k + 1)] for k in range(3)]
 
         load_w1(3, "picked_first")
         round_w1(round_on_gpsimd, 3)
         gains = held([P, 2, PACK], F32, "gains", after="w1_piece2")
         nc.sync.dma_start(gains[:], gain.rearrange("(a p t) -> p a t", a=2, t=PACK))
-        w3_s = held([P, 2, N], U8, "w3_s", after="picked_rest")
-        nc.vector.memset(w3_s[:].rearrange("p a c -> p (a c)").bitcast(I32), 0)
+        w3_s = w2_in_s[:, 0 : 2 * N].rearrange("p (a c) -> p a c", a=2)
         for r in range(4):
             nc.sync.dma_start(
                 w3_s[r:P:32, :, :].bitcast(I32), w3_scales[:, r:16:4, :].rearrange("a q c -> q a c").bitcast(I32)

@@ -22,6 +22,7 @@ PASS = P * PACK
 BLOCK = 128
 PAIR = 2 * BLOCK
 PIECE = 256
+PART = 64
 GROUP = 16
 ALIGN = 64
 STEPS = [(a, pair) for a in range(2) for pair in range(S // PAIR)]
@@ -282,9 +283,13 @@ def tile_list_lightning_flash_layers_kernel(
         finish(last - 1, None)
         h_q[step] = held([P, PAIR], U32, "h_q%d" % last)
         h_s[step] = held([P, PAIR], U8, "h_s%d" % last)
-        for entries in blocks:
+        part = held([P, PACK, PART], BF16, "part")
+        for t in range(PACK):
+            nc.scalar.activation(part[:, t, :], difference[last][:, 0, 0:PART, t], ACT.Copy, scale=gains[:, a, t : t + 1])
+        nc.scalar.copy(h_bf[step][:, 0:PART], part[:].rearrange("p t j -> p j t"))
+        for entries in (slice(BLOCK, PAIR), slice(PART, BLOCK)):
             apply_gain(nc.vector, last, entries)
-        for entries in blocks:
+        for entries in reversed(blocks):
             quantize_h(step, entries)
-        flash(pair, blocks[0], nc.sync, psum_a, "bank_a")
-        flash(pair, blocks[1], nc.scalar, psum_a, "bank_a")
+        flash(pair, blocks[1], nc.sync, psum_a, "bank_a")
+        flash(pair, blocks[0], nc.scalar, psum_a, "bank_a")

@@ -35,6 +35,7 @@ def tile_list_lightning_flash_layers_kernel(
     nc = tc.nc
     with ExitStack() as ctx:
         keep = ctx.enter_context(tc.tile_pool(name="keep", bufs=1))
+        shared = ctx.enter_context(tc.tile_pool(name="shared", bufs=1))
         work = ctx.enter_context(tc.tile_pool(name="work", bufs=LAG))
         psum_a = ctx.enter_context(tc.psum_pool(name="psum_a", bufs=2))
         psum_b = ctx.enter_context(tc.psum_pool(name="psum_b", bufs=4))
@@ -58,6 +59,15 @@ def tile_list_lightning_flash_layers_kernel(
         nc.gpsimd.memset(tab_s[:].bitcast(I32), 0)
         nc.sync.dma_start(tab_s[0:P:8, :].bitcast(I32), tab_scales[0].bitcast(I32))
 
+        w2_in_s = shared.tile([P, PASS], U8, name="w2_in_s", offset=4 * PAIR - PASS // 2, align_bytes=ALIGN)
+        nc.gpsimd.memset(w2_in_s[:].bitcast(I32), 0)
+
+        def load_w2_scales(queue, d):
+            rows = w2_scales[0, 4 * d : 4 * d + 4, :].rearrange("r (a c) -> a r c", a=2)
+            queue.dma_start(w2_in_s[32 * d : 32 * d + 8, :].bitcast(I32), rows.bitcast(I32))
+
+        load_w2_scales(nc.sync, 2)
+
         warm_in = held([P, 1], F32, "warm_in")
         warm_out = held([P, 1], F32, "warm_out")
         nc.vector.memset(warm_in[:], 1.0)
@@ -67,7 +77,9 @@ def tile_list_lightning_flash_layers_kernel(
         tab_w = held([P, T], U32, "tab_w")
         nc.sync.dma_start(tab_w[:].bitcast(I32), tab_words[0].rearrange("p t i -> p (t i)").bitcast(I32))
 
-        load_w1(2)
+        w2_in_w = held([P, 2 * H], U8, "w2_in_w")
+        nc.sync.dma_start(w2_in_w[:].bitcast(I32), w2_words[0].bitcast(I32))
+        load_w2_scales(nc.sync, 3)
 
         def gather_scales(name, start, stop):
             picked = held([P, stop - start], U8, name)
@@ -78,22 +90,17 @@ def tile_list_lightning_flash_layers_kernel(
             for r in rows:
                 nc.sync.dma_start(placed[r:P:32, :].bitcast(I32), picked[8 * r : P : 32, :].bitcast(I32))
 
-        first_s = held([P, PAIR], U8, "first_s")
+        first_s = held([P, 2 * PAIR], U8, "first_s")
         nc.gpsimd.memset(first_s[:].bitcast(I32), 0)
-        move_rows(first_s, gather_scales("picked_first", 0, PAIR), range(4))
-        picked_rest = gather_scales("picked_rest", PAIR, S)
+        move_rows(first_s, gather_scales("picked_first", 0, 2 * PAIR), range(4))
+        for d in range(2):
+            load_w2_scales(nc.gpsimd, d)
+        picked_rest = gather_scales("picked_rest", 2 * PAIR, S)
 
-        w2_in_w = held([P, 2 * H], U8, "w2_in_w", after="w1_piece1")
-        nc.sync.dma_start(w2_in_w[:].bitcast(I32), w2_words[0].bitcast(I32))
-        w2_in_s = held([P, H], U8, "w2_in_s")
-        nc.gpsimd.memset(w2_in_s[:].bitcast(I32), 0)
-        for r in range(4):
-            queue = nc.gpsimd if r < 3 else nc.sync
-            queue.dma_start(w2_in_s[r:P:32, :].bitcast(I32), w2_scales[0, r:16:4, :].bitcast(I32))
+        gains = held([P, 2, PACK], F32, "gains")
+        nc.gpsimd.dma_start(gains[:], gain.rearrange("(a p t) -> p a t", a=2, t=PACK))
 
-        rest_s = held([P, S - PAIR], U8, "rest_s")
-        nc.gpsimd.memset(rest_s[:].bitcast(I32), 0)
-        move_rows(rest_s, picked_rest, range(4))
+        load_w1(2, "w1_piece1")
 
         def gather_words(pair, picked):
             columns = slice(PAIR // GROUP * pair, PAIR // GROUP * (pair + 1))
@@ -104,10 +111,11 @@ def tile_list_lightning_flash_layers_kernel(
         w1_q = {}
         w1_s = [held([P, PASS], U8, "w1_s%d" % a) for a in range(2)]
 
-        def round_w1(copy, c):
+        def round_w1(copy, c, start=0, stop=PIECE):
             a, half = divmod(c, 2)
-            target = w1_bf[a][:, :, P // 2 * half : P // 2 * (half + 1), :]
-            copy(target.rearrange("p t m i -> p m t i"), w1_piece[c][:].rearrange("p i (m t) -> p m t i", t=PACK))
+            target = w1_bf[a][:, :, (PIECE * half + start) // PACK : (PIECE * half + stop) // PACK, :]
+            source = w1_piece[c][:, :, start:stop].rearrange("p i (m t) -> p m t i", t=PACK)
+            copy(target.rearrange("p t m i -> p m t i"), source)
 
         def round_on_gpsimd(target, source):
             nc.gpsimd.tensor_scalar(target, source, 1.0, 0.0, ALU.mult, ALU.add)
@@ -118,64 +126,59 @@ def tile_list_lightning_flash_layers_kernel(
                 out=w1_q[a][:].bitcast(FP8X4), scales=w1_s[a][:], in_=w1_bf[a][:].rearrange("p t m i -> p (t m i)")
             )
 
-        for c in range(3):
+        for c in range(2):
             round_w1(nc.scalar.copy, c)
         quantize_w1(0, None)
         first_w = gather_words(0, held([P, PAIR], U32, "v_w0")[:])
-        second_w = gather_words(1, held([P, PAIR], U32, "v_w1")[:])
-        w2_s = held([P, H], U8, "w2_s", after="w1_bf0")
-        w2_w = held([P, 2 * H], U8, "w2_w")
-        for a in range(2):
-            nc.vector.tensor_copy(
-                w2_s[:, PASS * a : PASS * (a + 1)].rearrange("p (t m) -> p t m", t=PACK),
-                w2_in_s[:, PASS * a : PASS * (a + 1)].rearrange("p (m t) -> p t m", t=PACK),
-            )
-            nc.vector.tensor_copy(
-                w2_w[:].bitcast(U16)[:, PASS * a : PASS * (a + 1)].rearrange("p (t m) -> p t m", t=PACK),
+        w2_s0 = held([P, PASS], U8, "w2_s0", after="w1_piece0")
+        nc.vector.tensor_copy(
+            w2_s0[:].rearrange("p (t m) -> p t m", t=PACK), w2_in_s[:].rearrange("p (m t) -> p t m", t=PACK)
+        )
+        w2_w = {}
+
+        def order_w2_words(copy, a, after):
+            w2_w[a] = held([P, 2 * PASS], U8, "w2_w%d" % a, after=after)
+            copy(
+                w2_w[a][:].bitcast(U16).rearrange("p (t m) -> p t m", t=PACK),
                 w2_in_w[:].bitcast(U16)[:, PASS * a : PASS * (a + 1)].rearrange("p (m t) -> p t m", t=PACK),
             )
-        rest_w = held([P, 2 * PAIR], U32, "v_w_rest", after="w1_piece1")
+
+        order_w2_words(nc.scalar.copy, 0, None)
+        second_w = gather_words(1, shared.tile([P, PAIR], U32, name="v_w1", offset=0, align_bytes=ALIGN)[:])
+        rest_w = shared.tile([P, 2 * PAIR], U32, name="v_w_rest", offset=4 * PAIR, align_bytes=ALIGN)
         nc.vector.tensor_copy(rest_w[:], tab_w[:].indirect(offsets[:, 2 * PAIR // GROUP : S // GROUP]))
         v_w = [first_w, second_w] + [rest_w[:, PAIR * k : PAIR * (k + 1)] for k in range(2)]
-        v_s = [first_s[:]] + [rest_s[:, PAIR * k : PAIR * (k + 1)] for k in range(3)]
 
-        load_w1(3, "picked_first")
-        round_w1(round_on_gpsimd, 3)
-        gains = held([P, 2, PACK], F32, "gains", after="w1_piece2")
-        nc.sync.dma_start(gains[:], gain.rearrange("(a p t) -> p a t", a=2, t=PACK))
-        w3_s = w2_in_s[:, 0 : 2 * N].rearrange("p (a c) -> p a c", a=2)
+        order_w2_words(nc.vector.tensor_copy, 1, "tab_w")
+        load_w1(3, "w1_bf0")
+        late_s = held([P, 3 * PASS], U8, "late_s", after="picked_first")
+        nc.gpsimd.memset(late_s[:].bitcast(I32), 0)
+        move_rows(late_s[:, 0:PASS], picked_rest, range(4))
+        v_s = [placed[:, PAIR * k : PAIR * (k + 1)] for placed in (first_s, late_s) for k in range(2)]
+        w2_s = [w2_s0[:], late_s[:, PASS : 2 * PASS]]
+        for c in (2, 3):
+            round_w1(round_on_gpsimd, c)
+        for d in range(4):
+            nc.sync.dma_start(w2_s[1][32 * d : 32 * d + 4, :].bitcast(I32), w2_s0[32 * d + 4 : 32 * d + 8, :].bitcast(I32))
+        w3_s = late_s[:, 2 * PASS : 3 * PASS].rearrange("p (a c) -> p a c", a=2)
         for r in range(4):
             nc.sync.dma_start(
                 w3_s[r:P:32, :, :].bitcast(I32), w3_scales[:, r:16:4, :].rearrange("a q c -> q a c").bitcast(I32)
             )
 
-        def products(a, pair, block):
-            rhs = v_w[pair][:, BLOCK * block : BLOCK * (block + 1)].bitcast(FP8X4)
-            rhs_scale = v_s[pair][:, BLOCK * block : BLOCK * (block + 1)]
-            bank_a = psum_a.tile([P, PACK, BLOCK], F32, name="bank_a")
-            bank_b = psum_b.tile([P, PACK, BLOCK], F32, name="bank_b")
+        def product(pool, name, words, width, dtype, scales, pair, block):
+            bank = pool.tile([P, PACK, BLOCK], F32, name=name)
             for t in range(PACK):
                 nc.tensor.matmul_mx(
-                    out=bank_a[:, t, :],
-                    lhsT=w1_q[a][:, P * t : P * (t + 1)].bitcast(FP8X4),
-                    lhsT_scale=w1_s[a][:, P * t : P * (t + 1)],
-                    rhs=rhs,
-                    rhs_scale=rhs_scale,
+                    out=bank[:, t, :],
+                    lhsT=words[:, width * P * t : width * P * (t + 1)].bitcast(dtype),
+                    lhsT_scale=scales[:, P * t : P * (t + 1)],
+                    rhs=v_w[pair][:, BLOCK * block : BLOCK * (block + 1)].bitcast(FP8X4),
+                    rhs_scale=v_s[pair][:, BLOCK * block : BLOCK * (block + 1)],
                     start=True,
                     stop=True,
                 )
-            for t in range(PACK):
-                c0 = PASS * a + P * t
-                nc.tensor.matmul_mx(
-                    out=bank_b[:, t, :],
-                    lhsT=w2_w[:, 2 * c0 : 2 * (c0 + P)].bitcast(FP4X4),
-                    lhsT_scale=w2_s[:, c0 : c0 + P],
-                    rhs=rhs,
-                    rhs_scale=rhs_scale,
-                    start=True,
-                    stop=True,
-                )
-            return bank_a[:], bank_b[:]
+            return bank[:]
 
         h_bf = {}
         h_q = {}
@@ -230,7 +233,9 @@ def tile_list_lightning_flash_layers_kernel(
         difference = {}
         for u, step in enumerate(STEPS):
             a, pair = step
-            banks = [products(a, pair, block) for block in range(2)]
+            banks_a = [product(psum_a, "bank_a", w1_q[a], 1, FP8X4, w1_s[a], pair, block) for block in range(2)]
+            banks_b = [product(psum_b, "bank_b", w2_w[a], 2, FP4X4, w2_s[a], pair, block) for block in range(2)]
+            banks = list(zip(banks_a, banks_b))
             for block in range(2):
                 if (u, block) != (last - 1, 0):
                     banks[block] = [bank.rearrange("p t j -> p j t") for bank in banks[block]]
@@ -238,10 +243,11 @@ def tile_list_lightning_flash_layers_kernel(
                     banks[block] = [bank.rearrange("p t (j e) -> p (t j) e", e=PACK) for bank in banks[block]]
             shape = [P, 2, BLOCK, PACK]
             logarithm = held(shape, F32, "logarithm%d" % u)
-            for block in range(2):
-                nc.scalar.activation(logarithm[:, block], banks[block][0], ACT.Square)
-            for block in range(2):
-                nc.scalar.activation(logarithm[:, block], logarithm[:, block], ACT.Ln, bias=1.0)
+            for group in [[0], [1]] if u == 0 else [[0, 1]]:
+                for block in group:
+                    nc.scalar.activation(logarithm[:, block], banks[block][0], ACT.Square)
+                for block in group:
+                    nc.scalar.activation(logarithm[:, block], logarithm[:, block], ACT.Ln, bias=1.0)
             if u == last:
                 break
             difference[u] = work.tile(shape, F32, name="difference")

@@ -111,11 +111,10 @@ def tile_list_lightning_flash_layers_kernel(
         w1_q = {}
         w1_s = [held([P, PASS], U8, "w1_s%d" % a) for a in range(2)]
 
-        def round_w1(copy, c, start=0, stop=PIECE):
+        def round_w1(copy, c, walk):
             a, half = divmod(c, 2)
-            target = w1_bf[a][:, :, (PIECE * half + start) // PACK : (PIECE * half + stop) // PACK, :]
-            source = w1_piece[c][:, :, start:stop].rearrange("p i (m t) -> p m t i", t=PACK)
-            copy(target.rearrange("p t m i -> p m t i"), source)
+            target = w1_bf[a][:, :, P // 2 * half : P // 2 * (half + 1), :]
+            copy(target.rearrange("p t m i -> " + walk), w1_piece[c][:].rearrange("p i (m t) -> " + walk, t=PACK))
 
         def round_on_gpsimd(target, source):
             nc.gpsimd.tensor_scalar(target, source, 1.0, 0.0, ALU.mult, ALU.add)
@@ -127,7 +126,7 @@ def tile_list_lightning_flash_layers_kernel(
             )
 
         for c in range(2):
-            round_w1(nc.scalar.copy, c)
+            round_w1(nc.scalar.copy, c, "p m i t")
         quantize_w1(0, None)
         first_w = gather_words(0, held([P, PAIR], U32, "v_w0")[:])
         w2_s0 = held([P, PASS], U8, "w2_s0", after="w1_piece0")
@@ -157,7 +156,7 @@ def tile_list_lightning_flash_layers_kernel(
         v_s = [placed[:, PAIR * k : PAIR * (k + 1)] for placed in (first_s, late_s) for k in range(2)]
         w2_s = [w2_s0[:], late_s[:, PASS : 2 * PASS]]
         for c in (2, 3):
-            round_w1(round_on_gpsimd, c)
+            round_w1(round_on_gpsimd, c, "p m t i")
         for d in range(4):
             nc.sync.dma_start(w2_s[1][32 * d : 32 * d + 4, :].bitcast(I32), w2_s0[32 * d + 4 : 32 * d + 8, :].bitcast(I32))
         w3_s = late_s[:, 2 * PASS : 3 * PASS].rearrange("p (a c) -> p a c", a=2)

@@ -59,7 +59,7 @@ def tile_list_lightning_flash_layers_kernel(
         nc.gpsimd.memset(tab_s[:].bitcast(I32), 0)
         nc.sync.dma_start(tab_s[0:P:8, :].bitcast(I32), tab_scales[0].bitcast(I32))
 
-        w2_in_s = shared.tile([P, PASS], U8, name="w2_in_s", offset=4 * PAIR - PASS // 2, align_bytes=ALIGN)
+        w2_in_s = shared.tile([P, PASS], U8, name="w2_in_s", offset=0, align_bytes=ALIGN)
         nc.gpsimd.memset(w2_in_s[:].bitcast(I32), 0)
 
         def load_w2_scales(queue, d):
@@ -77,7 +77,7 @@ def tile_list_lightning_flash_layers_kernel(
         tab_w = held([P, T], U32, "tab_w")
         nc.sync.dma_start(tab_w[:].bitcast(I32), tab_words[0].rearrange("p t i -> p (t i)").bitcast(I32))
 
-        w2_in_w = held([P, 2 * H], U8, "w2_in_w")
+        w2_in_w = shared.tile([P, 2 * H], U8, name="w2_in_w", offset=4 * PAIR, align_bytes=ALIGN)
         nc.sync.dma_start(w2_in_w[:].bitcast(I32), w2_words[0].bitcast(I32))
         load_w2_scales(nc.sync, 3)
 
@@ -129,10 +129,6 @@ def tile_list_lightning_flash_layers_kernel(
             round_w1(nc.scalar.copy, c, "p m i t")
         quantize_w1(0, None)
         first_w = gather_words(0, held([P, PAIR], U32, "v_w0")[:])
-        w2_s0 = held([P, PASS], U8, "w2_s0", after="w1_piece0")
-        nc.vector.tensor_copy(
-            w2_s0[:].rearrange("p (t m) -> p t m", t=PACK), w2_in_s[:].rearrange("p (m t) -> p t m", t=PACK)
-        )
         w2_w = {}
 
         def order_w2_words(copy, a, after):
@@ -143,12 +139,16 @@ def tile_list_lightning_flash_layers_kernel(
             )
 
         order_w2_words(nc.scalar.copy, 0, None)
+        order_w2_words(nc.vector.tensor_copy, 1, None)
+        w2_s0 = held([P, PASS], U8, "w2_s0", after="w1_piece0")
+        nc.vector.tensor_copy(
+            w2_s0[:].rearrange("p (t m) -> p t m", t=PACK), w2_in_s[:].rearrange("p (m t) -> p t m", t=PACK)
+        )
         second_w = gather_words(1, shared.tile([P, PAIR], U32, name="v_w1", offset=0, align_bytes=ALIGN)[:])
         rest_w = shared.tile([P, 2 * PAIR], U32, name="v_w_rest", offset=4 * PAIR, align_bytes=ALIGN)
         nc.vector.tensor_copy(rest_w[:], tab_w[:].indirect(offsets[:, 2 * PAIR // GROUP : S // GROUP]))
         v_w = [first_w, second_w] + [rest_w[:, PAIR * k : PAIR * (k + 1)] for k in range(2)]
 
-        order_w2_words(nc.vector.tensor_copy, 1, "tab_w")
         load_w1(3, "w1_bf0")
         late_s = held([P, 3 * PASS], U8, "late_s", after="picked_first")
         nc.gpsimd.memset(late_s[:].bitcast(I32), 0)

@@ -21,7 +21,7 @@ PACK = 4
 PASS = P * PACK
 BLOCK = 128
 PAIR = 2 * BLOCK
-PIECE = 256
+CUTS = (0, 320, 512, 768, 1024)
 PART = 64
 GROUP = 16
 ALIGN = 64
@@ -49,8 +49,8 @@ def tile_list_lightning_flash_layers_kernel(
         w1_piece = {}
 
         def load_w1(c, after=None):
-            w1_piece[c] = held([P, PACK, PIECE], F32, "w1_piece%d" % c, after=after)
-            nc.sync.dma_start(w1_piece[c][:], w1_rows[:, :, PIECE * c : PIECE * (c + 1)])
+            w1_piece[c] = held([P, PACK, CUTS[c + 1] - CUTS[c]], F32, "w1_piece%d" % c, after=after)
+            nc.sync.dma_start(w1_piece[c][:], w1_rows[:, :, CUTS[c] : CUTS[c + 1]])
 
         load_w1(0)
         nc.sync.dma_start(offsets[:], offs)
@@ -112,8 +112,8 @@ def tile_list_lightning_flash_layers_kernel(
         w1_s = [held([P, PASS], U8, "w1_s%d" % a) for a in range(2)]
 
         def round_w1(copy, c, walk):
-            a, half = divmod(c, 2)
-            target = w1_bf[a][:, :, P // 2 * half : P // 2 * (half + 1), :]
+            a = c // 2
+            target = w1_bf[a][:, :, (CUTS[c] - PASS * a) // PACK : (CUTS[c + 1] - PASS * a) // PACK, :]
             copy(target.rearrange("p t m i -> " + walk), w1_piece[c][:].rearrange("p i (m t) -> " + walk, t=PACK))
 
         def round_on_gpsimd(target, source):

from contextlib import ExitStack

import concourse.mybir as mybir

K, T, S, H, N = 512, 2048, 1024, 1024, 256
FLOPS = 2 * (2 * K * H * S) + 2 * H * N * S

F32 = mybir.dt.float32
BF16 = mybir.dt.bfloat16
I32 = mybir.dt.int32
U32 = mybir.dt.uint32
U16 = mybir.dt.uint16
U8 = mybir.dt.uint8
FP8X4 = mybir.dt.float8_e4m3fn_x4
FP4X4 = mybir.dt.float4_e2m1fn_x4
ACT = mybir.ActivationFunctionType
ALU = mybir.AluOpType

P = 128
PACK = 4
PASS = P * PACK
BLOCK = 128
PAIR = 2 * BLOCK
CUTS = (0, 320, 512, 768, 1024)
PART = 64
GROUP = 16
ALIGN = 64
STEPS = [(a, pair) for a in range(2) for pair in range(S // PAIR)]
LAG = 2


def tile_list_lightning_flash_layers_kernel(
    tc, tab_words, tab_scales, offs, w1, w2_words, w2_scales, w3_words, w3_scales, gain, out
):
    nc = tc.nc
    with ExitStack() as ctx:
        keep = ctx.enter_context(tc.tile_pool(name="keep", bufs=1))
        shared = ctx.enter_context(tc.tile_pool(name="shared", bufs=1))
        work = ctx.enter_context(tc.tile_pool(name="work", bufs=LAG))
        psum_a = ctx.enter_context(tc.psum_pool(name="psum_a", bufs=2))
        psum_b = ctx.enter_context(tc.psum_pool(name="psum_b", bufs=4))
        psum_y = ctx.enter_context(tc.psum_pool(name="psum_y", bufs=2))

        def held(shape, dtype, name, after=None):
            return keep.tile(shape, dtype, name=name, tag=after or name, align_bytes=ALIGN)

        offsets = keep.tile([P, S // GROUP], U16, name="offsets")
        w1_rows = w1.rearrange("(p i) c -> p i c", i=PACK)
        w1_piece = {}

        def load_w1(c, after=None):
            w1_piece[c] = held([P, PACK, CUTS[c + 1] - CUTS[c]], F32, "w1_piece%d" % c, after=after)
            nc.sync.dma_start(w1_piece[c][:], w1_rows[:, :, CUTS[c] : CUTS[c + 1]])

        load_w1(0)
        nc.sync.dma_start(offsets[:], offs)

        tab_s = held([P, T], U8, "tab_s")
        nc.gpsimd.memset(tab_s[:].bitcast(I32), 0)
        nc.sync.dma_start(tab_s[0:P:8, :].bitcast(I32), tab_scales[0].bitcast(I32))

        w2_in_s = shared.tile([P, PASS], U8, name="w2_in_s", offset=0, align_bytes=ALIGN)
        nc.gpsimd.memset(w2_in_s[:].bitcast(I32), 0)

        def load_w2_scales(queue, d):
            rows = w2_scales[0, 4 * d : 4 * d + 4, :].rearrange("r (a c) -> a r c", a=2)
            queue.dma_start(w2_in_s[32 * d : 32 * d + 8, :].bitcast(I32), rows.bitcast(I32))

        load_w2_scales(nc.sync, 2)

        warm_in = held([P, 1], F32, "warm_in")
        warm_out = held([P, 1], F32, "warm_out")
        nc.vector.memset(warm_in[:], 1.0)
        nc.scalar.activation(warm_out[:], warm_in[:], ACT.Ln)

        load_w1(1)
        tab_w = held([P, T], U32, "tab_w")
        nc.sync.dma_start(tab_w[:].bitcast(I32), tab_words[0].rearrange("p t i -> p (t i)").bitcast(I32))

        w2_in_w = shared.tile([P, 2 * H], U8, name="w2_in_w", offset=4 * PAIR, align_bytes=ALIGN)
        nc.sync.dma_start(w2_in_w[:].bitcast(I32), w2_words[0].bitcast(I32))
        load_w2_scales(nc.sync, 3)

        def gather_scales(name, start, stop):
            picked = held([P, stop - start], U8, name)
            nc.vector.tensor_copy(picked[:], tab_s[:].indirect(offsets[:, start // GROUP : stop // GROUP]))
            return picked

        def move_rows(placed, picked, rows):
            for r in rows:
                nc.sync.dma_start(placed[r:P:32, :].bitcast(I32), picked[8 * r : P : 32, :].bitcast(I32))

        first_s = held([P, 2 * PAIR], U8, "first_s")
        nc.gpsimd.memset(first_s[:].bitcast(I32), 0)
        move_rows(first_s, gather_scales("picked_first", 0, 2 * PAIR), range(4))
        for d in range(2):
            load_w2_scales(nc.gpsimd, d)
        picked_rest = gather_scales("picked_rest", 2 * PAIR, S)

        gains = held([P, 2, PACK], F32, "gains")
        nc.gpsimd.dma_start(gains[:], gain.rearrange("(a p t) -> p a t", a=2, t=PACK))

        load_w1(2, "w1_piece1")

        def gather_words(pair, picked):
            columns = slice(PAIR // GROUP * pair, PAIR // GROUP * (pair + 1))
            nc.vector.tensor_copy(picked, tab_w[:].indirect(offsets[:, columns]))
            return picked

        w1_bf = [held([P, PACK, P, PACK], BF16, "w1_bf%d" % a) for a in range(2)]
        w1_q = {}
        w1_s = [held([P, PASS], U8, "w1_s%d" % a) for a in range(2)]

        def round_w1(copy, c, walk):
            a = c // 2
            target = w1_bf[a][:, :, (CUTS[c] - PASS * a) // PACK : (CUTS[c + 1] - PASS * a) // PACK, :]
            copy(target.rearrange("p t m i -> " + walk), w1_piece[c][:].rearrange("p i (m t) -> " + walk, t=PACK))

        def round_on_gpsimd(target, source):
            nc.gpsimd.tensor_scalar(target, source, 1.0, 0.0, ALU.mult, ALU.add)

        def quantize_w1(a, after):
            w1_q[a] = held([P, PASS], U32, "w1_q%d" % a, after=after)
            nc.vector.quantize_mx(
                out=w1_q[a][:].bitcast(FP8X4), scales=w1_s[a][:], in_=w1_bf[a][:].rearrange("p t m i -> p (t m i)")
            )

        for c in range(2):
            round_w1(nc.scalar.copy, c, "p m i t")
        quantize_w1(0, None)
        first_w = gather_words(0, held([P, PAIR], U32, "v_w0")[:])
        w2_w = {}

        def order_w2_words(copy, a, after):
            w2_w[a] = held([P, 2 * PASS], U8, "w2_w%d" % a, after=after)
            copy(
                w2_w[a][:].bitcast(U16).rearrange("p (t m) -> p t m", t=PACK),
                w2_in_w[:].bitcast(U16)[:, PASS * a : PASS * (a + 1)].rearrange("p (m t) -> p t m", t=PACK),
            )

        order_w2_words(nc.scalar.copy, 0, None)
        order_w2_words(nc.vector.tensor_copy, 1, None)
        w2_s0 = held([P, PASS], U8, "w2_s0", after="w1_piece0")
        nc.vector.tensor_copy(
            w2_s0[:].rearrange("p (t m) -> p t m", t=PACK), w2_in_s[:].rearrange("p (m t) -> p t m", t=PACK)
        )
        second_w = gather_words(1, shared.tile([P, PAIR], U32, name="v_w1", offset=0, align_bytes=ALIGN)[:])
        rest_w = shared.tile([P, 2 * PAIR], U32, name="v_w_rest", offset=4 * PAIR, align_bytes=ALIGN)
        nc.vector.tensor_copy(rest_w[:], tab_w[:].indirect(offsets[:, 2 * PAIR // GROUP : S // GROUP]))
        v_w = [first_w, second_w] + [rest_w[:, PAIR * k : PAIR * (k + 1)] for k in range(2)]

        load_w1(3, "w1_bf0")
        late_s = held([P, 3 * PASS], U8, "late_s", after="picked_first")
        nc.gpsimd.memset(late_s[:].bitcast(I32), 0)
        move_rows(late_s[:, 0:PASS], picked_rest, range(4))
        v_s = [placed[:, PAIR * k : PAIR * (k + 1)] for placed in (first_s, late_s) for k in range(2)]
        w2_s = [w2_s0[:], late_s[:, PASS : 2 * PASS]]
        for c in (2, 3):
            round_w1(round_on_gpsimd, c, "p m t i")
        for d in range(4):
            nc.sync.dma_start(w2_s[1][32 * d : 32 * d + 4, :].bitcast(I32), w2_s0[32 * d + 4 : 32 * d + 8, :].bitcast(I32))
        w3_s = late_s[:, 2 * PASS : 3 * PASS].rearrange("p (a c) -> p a c", a=2)
        for r in range(4):
            nc.sync.dma_start(
                w3_s[r:P:32, :, :].bitcast(I32), w3_scales[:, r:16:4, :].rearrange("a q c -> q a c").bitcast(I32)
            )

        def product(pool, name, words, width, dtype, scales, pair, block):
            bank = pool.tile([P, PACK, BLOCK], F32, name=name)
            for t in range(PACK):
                nc.tensor.matmul_mx(
                    out=bank[:, t, :],
                    lhsT=words[:, width * P * t : width * P * (t + 1)].bitcast(dtype),
                    lhsT_scale=scales[:, P * t : P * (t + 1)],
                    rhs=v_w[pair][:, BLOCK * block : BLOCK * (block + 1)].bitcast(FP8X4),
                    rhs_scale=v_s[pair][:, BLOCK * block : BLOCK * (block + 1)],
                    start=True,
                    stop=True,
                )
            return bank[:]

        h_bf = {}
        h_q = {}
        h_s = {}

        def quantize_h(step, entries):
            nc.vector.quantize_mx(
                out=h_q[step][:, entries].bitcast(FP8X4),
                scales=h_s[step][:, entries],
                in_=h_bf[step][:, entries, :].rearrange("p j t -> p (j t)"),
            )

        out_rows = out.rearrange("(c p) j -> p c j", p=P)

        def flash(pair, entries, queue, pool, tag):
            width = entries.stop - entries.start
            bank_y = pool.tile([P, 2, width], F32, name="bank_y", tag=tag)
            for a in range(2):
                for c in range(2):
                    nc.tensor.matmul_mx(
                        out=bank_y[:, c, :],
                        lhsT=w3_w[:, a, P * c : P * (c + 1)].bitcast(FP8X4),
                        lhsT_scale=w3_s[:, a, P * c : P * (c + 1)],
                        rhs=h_q[(a, pair)][:, entries].bitcast(FP8X4),
                        rhs_scale=h_s[(a, pair)][:, entries],
                        start=(a, c) == (0, 0),
                        stop=(a, c) == (1, 1),
                    )
            squared = held([P, 2, width], F32, "squared%d_%d" % (pair, entries.start))
            nc.scalar.activation(squared[:], bank_y[:], ACT.Square)
            j0 = PAIR * pair + entries.start
            queue.dma_start(out_rows[:, :, j0 : j0 + width], squared[:])

        whole = slice(0, PAIR)
        blocks = [slice(0, BLOCK), slice(BLOCK, PAIR)]
        last = len(STEPS) - 1

        def finish(u, after):
            step = STEPS[u]
            h_q[step] = held([P, PAIR], U32, "h_q%d" % u, after=after)
            h_s[step] = held([P, PAIR], U8, "h_s%d" % u)
            quantize_h(step, whole)
            if step[0] == 1:
                flash(step[1], whole, nc.sync, psum_y, "bank_y")

        def apply_gain(engine, u, entries):
            a = STEPS[u][0]
            by_slot = gains[:, a : a + 1, :].broadcast_to([P, entries.stop - entries.start, PACK])
            flat = difference[u][:].rearrange("p b j t -> p (b j) t")
            engine.tensor_tensor(h_bf[STEPS[u]][:, entries], flat[:, entries], by_slot, ALU.mult)

        difference = {}
        for u, step in enumerate(STEPS):
            a, pair = step
            banks_a = [product(psum_a, "bank_a", w1_q[a], 1, FP8X4, w1_s[a], pair, block) for block in range(2)]
            banks_b = [product(psum_b, "bank_b", w2_w[a], 2, FP4X4, w2_s[a], pair, block) for block in range(2)]
            banks = list(zip(banks_a, banks_b))
            for block in range(2):
                if (u, block) != (last - 1, 0):
                    banks[block] = [bank.rearrange("p t j -> p j t") for bank in banks[block]]
                else:
                    banks[block] = [bank.rearrange("p t (j e) -> p (t j) e", e=PACK) for bank in banks[block]]
            shape = [P, 2, BLOCK, PACK]
            logarithm = held(shape, F32, "logarithm%d" % u)
            for group in [[0], [1]] if u == 0 else [[0, 1]]:
                for block in group:
                    nc.scalar.activation(logarithm[:, block], banks[block][0], ACT.Square)
                for block in group:
                    nc.scalar.activation(logarithm[:, block], logarithm[:, block], ACT.Ln, bias=1.0)
            if u == last:
                break
            difference[u] = work.tile(shape, F32, name="difference")
            for block in range(2):
                nc.vector.scalar_tensor_tensor(
                    difference[u][:, block], banks[block][1], 0.0, logarithm[:, block], ALU.max, ALU.subtract
                )
            for block in range(2):
                nc.vector.scalar_tensor_tensor(
                    difference[u][:, block], banks[block][1], 0.0, difference[u][:, block], ALU.min, ALU.subtract
                )
            if u == 0:
                w3_w = held([P, 2, N], U32, "w3_w", after="logarithm0")
                nc.sync.dma_start(w3_w[:].bitcast(I32), w3_words.rearrange("a p c i -> p a (c i)").bitcast(I32))
            if u == LAG - 1:
                quantize_w1(1, "logarithm%d" % u)
            if u >= LAG:
                finish(u - LAG, "logarithm%d" % u)
            if u < last - 1:
                h_bf[step] = held([P, PAIR, PACK], BF16, "h_bf%d" % u)
                for entries in blocks if u == 0 else [whole]:
                    apply_gain(nc.gpsimd, u, entries)

        loss = held([P, 2, BLOCK, PACK], F32, "loss")
        for block in range(2):
            nc.scalar.activation(loss[:, block], banks[block][1], ACT.Abs)
        by_slot = difference[last - 1][:, 0].rearrange("p (t j) e -> p t (j e)", t=PACK)
        by_slot_bf = held([P, PACK, BLOCK], BF16, "by_slot_bf")
        for t in range(PACK):
            nc.scalar.activation(by_slot_bf[:, t, :], by_slot[:, t, :], ACT.Copy, scale=gains[:, a, t : t + 1])
        h_bf[STEPS[last - 1]] = held([P, PAIR, PACK], BF16, "h_bf%d" % (last - 1))
        nc.scalar.copy(h_bf[STEPS[last - 1]][:, blocks[0]], by_slot_bf[:].rearrange("p t j -> p j t"))
        finish(last - 2, None)
        apply_gain(nc.vector, last - 1, blocks[1])
        difference[last] = held([P, 2, BLOCK, PACK], F32, "difference_last", after="h_bf%d" % (last - 3))
        h_bf[step] = held([P, PAIR, PACK], BF16, "h_bf%d" % last)
        for block in range(2):
            nc.vector.tensor_tensor(difference[last][:, block], logarithm[:, block], loss[:, block], ALU.subtract)
        finish(last - 1, None)
        h_q[step] = held([P, PAIR], U32, "h_q%d" % last)
        h_s[step] = held([P, PAIR], U8, "h_s%d" % last)
        part = held([P, PACK, PART], BF16, "part")
        for t in range(PACK):
            nc.scalar.activation(part[:, t, :], difference[last][:, 0, 0:PART, t], ACT.Copy, scale=gains[:, a, t : t + 1])
        nc.scalar.copy(h_bf[step][:, 0:PART], part[:].rearrange("p t j -> p j t"))
        for entries in (slice(BLOCK, PAIR), slice(PART, BLOCK)):
            apply_gain(nc.vector, last, entries)
        for entries in reversed(blocks):
            quantize_h(step, entries)
        flash(pair, blocks[1], nc.sync, psum_a, "bank_a")
        flash(pair, blocks[0], nc.scalar, psum_a, "bank_a")
